import numpy as np
import ml_dtypes


def mxq(x, axis, fmt="e4m3"):
    dtype, down = {"e4m3": (ml_dtypes.float8_e4m3fn, 7), "e5m2": (ml_dtypes.float8_e5m2, 14)}[fmt]
    v = np.moveaxis(np.asarray(x, np.float32).astype(ml_dtypes.bfloat16).astype(np.float64), axis, -1)
    blocks = v.reshape(v.shape[:-1] + (-1, 32))
    amax = np.abs(blocks).max(-1, keepdims=True)
    byte = np.maximum(np.where(amax > 0, np.frexp(amax)[1] - 1 + 127, 0) - down, 1)
    scale = np.exp2(byte - 127.0)
    codes = (blocks / scale).astype(np.float32).astype(dtype).astype(np.float64)
    return np.moveaxis((codes * scale).reshape(v.shape), -1, axis)


WIDE = False


def mx_kscale(k):
    if not WIDE:
        return np.ones(k)
    levels = np.array([10, -10, 5, -5, 0])
    if k % 512:
        return np.exp2(np.random.permutation(np.resize(levels, k // 32))).repeat(32)
    a = np.empty((k // 512, 16))
    for p in range(k // 512):
        a[p, :8] = np.random.permutation(np.resize(levels, 8))
        for g in range(8):
            far = levels[np.abs(levels - a[p, g]) >= 10]
            a[p, g + 8] = far[np.random.randint(len(far))]
    return np.exp2(a.ravel()).repeat(32)


BF16 = ml_dtypes.bfloat16


def bf(x):
    return np.asarray(x, np.float32).astype(BF16)


def f64(x):
    return np.asarray(x).astype(np.float64)


E2M1 = np.array([0.0, 0.5, 1.0, 1.5, 2.0, 3.0, 4.0, 6.0, -0.0, -0.5, -1.0, -1.5, -2.0, -3.0, -4.0, -6.0])


def pack_weight(w, fmt):
    k, n = w.shape
    w = f64(bf(w)).reshape(k // 32, 32, n)
    amax = np.abs(w).max(1)
    if fmt == "e4m3":
        byte = np.frexp(amax)[1] - 1 + 127 - 7
    else:
        mant, ex = np.frexp(amax / 6.0)
        byte = np.where(mant > 0.5, ex, ex - 1) + 127
    byte = np.clip(np.where(amax > 0, byte, 1), 1, 254)
    scaled = (w * np.exp2(127.0 - byte)[:, None, :]).reshape(k, n).astype(np.float32)
    by_word = np.ascontiguousarray(scaled.reshape(k // 512, 128, 4, n).transpose(0, 1, 3, 2))
    if fmt == "e4m3":
        words = by_word.astype(ml_dtypes.float8_e4m3fn).view(np.uint8)
    else:
        c = by_word.astype(ml_dtypes.float4_e2m1fn).view(np.uint8) & 0xF
        words = c[..., 0::2] | (c[..., 1::2] << 4)
    return np.ascontiguousarray(words), np.ascontiguousarray(byte.astype(np.uint8).reshape(k // 512, 16, n))


def unpack_weight(words, scales, fmt):
    g, p, n, _ = words.shape
    if fmt == "e4m3":
        vals = np.ascontiguousarray(words).view(ml_dtypes.float8_e4m3fn).astype(np.float64)
    else:
        nib = np.empty((g, p, n, 4), np.uint8)
        nib[..., 0::2] = words & 0xF
        nib[..., 1::2] = words >> 4
        vals = E2M1[nib]
    vals = vals * np.repeat(np.exp2(scales.astype(np.float64) - 127.0), 8, axis=1)[..., None]
    return vals.transpose(0, 1, 3, 2).reshape(g * 512, n)
def pack4(w):
    words, scales = pack_weight(w, "e2m1")
    return words.reshape(words.shape[0], 128, -1), scales


def unpack4(words, scales):
    return unpack_weight(words.reshape(words.shape[0], 128, -1, 2), scales, "e2m1")


def planes(Y):
    n, m = Y.shape
    b = f64(bf(Y)).reshape(n // 32, 32, m)
    amax = np.abs(b).max(1)
    byte = np.clip(np.where(amax > 0, np.frexp(amax)[1] - 1 + 127 - 7, 1), 1, 254)
    codes = (b * np.exp2(127.0 - byte)[:, None, :]).reshape(n, m).astype(np.float32).astype(ml_dtypes.float8_e4m3fn).view(np.uint8)
    words = codes.reshape(n // 512, 128, 4, m).transpose(0, 1, 3, 2)
    return np.ascontiguousarray(words), np.ascontiguousarray(byte.astype(np.uint8).reshape(n // 512, 16, m))


T, DO, DR, Q, H, N = 1024, 512, 1536, 1024, 512, 2048

def setup_inputs():
    so, sr, t = mx_kscale(DO), mx_kscale(DR), mx_kscale(Q)
    xo = 3.0 * np.random.randn(T, DO)
    xr = np.random.randn(T, DR)
    wo = 0.7 * np.random.randn(DO, Q) / np.sqrt(DO + DR)
    wr = 0.7 * np.random.randn(DR, Q) / np.sqrt(DO + DR)
    bq = 0.3 * np.random.randn(Q)
    sub = np.random.randn(Q, N) / np.sqrt(H)
    gain = 4.0 * np.exp(0.8 * np.random.randn(N))
    wr_words, wr_scales = pack4(wr * t / sr[:, None])
    sub_words, sub_scales = pack_weight(sub / t[:, None], "e4m3")
    return {"xo": bf(xo * so), "xr": bf(xr * sr), "wo": bf(wo * t / so[:, None]),
            "wr_words": wr_words, "wr_scales": wr_scales, "bq": bf(bq * t),
            "sub_words": sub_words, "sub_scales": sub_scales, "gain": bf(gain)}

def reference(xo, xr, wo, wr_words, wr_scales, bq, sub_words, sub_scales, gain):
    wr = unpack4(wr_words, wr_scales)
    sub = unpack_weight(sub_words, sub_scales, "e4m3")
    u = (mxq(f64(xo), 1, "e4m3") @ mxq(f64(wo), 0, "e4m3")) + (mxq(f64(xr), 1, "e4m3") @ wr) + f64(bq)
    uq = mxq(u, 1, "e4m3")
    a1 = uq[:, :H] @ sub[:H]
    a2 = uq[:, H:] @ sub[H:]
    y = 1.0 / (1.0 + np.exp(-a1)) * (1.0 / (1.0 + np.exp(-a2))) * f64(gain)
    Y = y.T
    words, scales = planes(Y)
    return y, words, scales

@@ -1,0 +1,494 @@
+from contextlib import ExitStack
+
+import concourse.mybir as mybir
+from concourse.masks import make_identity
+
+T, DO, DR, Q, H, N = 1024, 512, 1536, 1024, 512, 2048
+FLOPS = 2 * T * (DO + DR) * Q + 2 * T * Q * N
+
+F32 = mybir.dt.float32
+BF16 = mybir.dt.bfloat16
+I32 = mybir.dt.int32
+U32 = mybir.dt.uint32
+U8 = mybir.dt.uint8
+FP8X4 = mybir.dt.float8_e4m3fn_x4
+FP4X4 = mybir.dt.float4_e2m1fn_x4
+ALU = mybir.AluOpType
+ACT = mybir.ActivationFunctionType
+
+P = 128
+KP = 512
+BANK = 512
+TILES = T // P
+XG = (DO + DR) // KP
+CHUNKS = N // BANK
+HALF = N // 2
+GP = 0
+ACT_CAST = 1
+XA = [99,99,4,5,6,6,6,6]
+XB = [99,99,4,5,5,5,5,5]
+SA = [99,2,2,3,3,3,3,3]
+SB = [99,2,2,2,2,2,2,2]
+UT = [99,1,2,2,2,2,2,2]
+LY = 2
+ACT_FROM = 15
+GDMA = 1
+ACT_EVERY = 2
+POOL = 0
+SHALLOW = 1
+FIRST = 0
+S2FIRST = [0]
+
+
+def tile_paired_subkey_router_k6_kernel(
+    tc, xo, xr, wo, wr_words, wr_scales, bq, sub_words, sub_scales, gain, out_0, out_1, out_2
+):
+    nc = tc.nc
+    with ExitStack() as ctx:
+        keep = ctx.enter_context(tc.tile_pool(name="keep", bufs=1))
+        work = ctx.enter_context(tc.tile_pool(name="work", bufs=2))
+        psum = ctx.enter_context(tc.psum_pool(name="psum", bufs=1))
+        ctx.enter_context(tc.manual_schedule())
+
+        def bank(dtype=F32, width=BANK):
+            return psum.tile([P, width], dtype, name="bank", tag="bank", bufs=4 if GP else 6)
+
+        ident32 = keep.tile([P, P], F32, name="ident32")
+        ident16 = keep.tile([P, P], BF16, name="ident16")
+        vec_rows = keep.tile([P, P], BF16, name="vec_rows")
+        wr_plane = keep.tile([P, XG - 1, Q], U8, name="wr_plane", align_bytes=64)
+        sub_plane = keep.tile([P, N], U8, name="sub_plane", align_bytes=64)
+        nc.gpsimd.memset(vec_rows[:], 0.0)
+        nc.vector.memset(wr_plane[:].rearrange("p g n -> p (g n)").bitcast(I32), 0)
+        nc.vector.memset(sub_plane[:].bitcast(I32), 0)
+
+        xo_sb = [keep.tile([P, DO], BF16, name="xo%d" % i) for i in range(TILES)]
+        xr_sb = [keep.tile([P, DR], BF16, name="xr%d" % i) for i in range(TILES)]
+        wo_raw = [keep.tile([P, 4, H], BF16, name="wo_raw%d" % h) for h in range(2)]
+        wr_codes = [keep.tile([P, XG - 1, 2 * H], U8, name="wr_codes%d" % h, align_bytes=64) for h in range(2)]
+        sub_codes = [keep.tile([P, 2, BANK], U32, name="sub_codes%d" % c, align_bytes=64) for c in range(CHUNKS)]
+
+        def load_x(i):
+            rows = slice(i * P, (i + 1) * P)
+            nc.sync.dma_start(out=xo_sb[i][:], in_=xo[rows, :])
+            nc.sync.dma_start(out=xr_sb[i][:], in_=xr[rows, :])
+
+        def load_sub(c):
+            cols = sub_words.rearrange("g p n t -> p g (n t)")[:, :, 4 * BANK * c : 4 * BANK * (c + 1)]
+            nc.sync.dma_start(out=sub_codes[c][:].bitcast(I32), in_=cols.bitcast(I32))
+
+        def load_wo(h):
+            nc.sync.dma_start(
+                out=wo_raw[h][:], in_=wo[:, h * H : (h + 1) * H].rearrange("(p j) n -> p j n", j=4)
+            )
+
+        def load_wr(h):
+            nc.sync.dma_start(
+                out=wr_codes[h][:].bitcast(I32),
+                in_=wr_words[:, :, 2 * H * h : 2 * H * (h + 1)].rearrange("g p b -> p g b").bitcast(I32),
+            )
+
+        nc.gpsimd.dma_start(out=vec_rows[0 : Q // P, :], in_=bq.rearrange("(c p) -> c p", p=P))
+        if not GDMA:
+            nc.gpsimd.dma_start(out=vec_rows[Q // P : (Q + N) // P, :], in_=gain.rearrange("(c p) -> c p", p=P))
+        make_identity(nc, ident32[:])
+        make_identity(nc, ident16[:])
+        load_x(0)
+        load_wo(0)
+        load_wr(0)
+        for q in range(4):
+            nc.sync.dma_start(
+                out=wr_plane[32 * q : 32 * q + 4, :, :].bitcast(I32),
+                in_=wr_scales[:, 4 * q : 4 * q + 4, :].rearrange("g r n -> r g n").bitcast(I32),
+            )
+        if SHALLOW:
+            load_wo(1)
+            load_wr(1)
+            load_x(1)
+        else:
+            load_x(1)
+            load_wo(1)
+            load_wr(1)
+        load_sub(0)
+        load_sub(1)
+        for q in range(4):
+            nc.sync.dma_start(
+                out=sub_plane[32 * q : 32 * q + 8, :].bitcast(I32),
+                in_=sub_scales[:, 4 * q : 4 * q + 4, :].bitcast(I32),
+            )
+        load_x(2)
+        load_sub(2)
+        load_sub(3)
+        gain_bc = keep.tile([P, N], BF16, name="gain_bc")
+        gain_of = {}
+        for i in range(3, TILES):
+            load_x(i)
+            if i == 3 and GDMA:
+                nc.sync.dma_start(out=gain_bc[:], in_=gain.partition_broadcast(P))
+                for h in range(2):
+                    gain_of[h] = gain_bc[:, h * HALF : (h + 1) * HALF]
+
+        bias_bc = keep.tile([P, Q], BF16, name="bias_bc")
+
+        def turn_vector(rows):
+            acc = bank(BF16, 2 * BANK)
+            nc.tensor.transpose(acc[:, 0:P], rows[:], ident16[:])
+            cols = work.tile([P, P], BF16, name="vec_cols")
+            nc.scalar.copy(out=cols[:], in_=acc[:, 0:P])
+            return cols
+
+        def spread(cols, first_col, acc):
+            for c in range(2 * BANK // P):
+                col = cols[:, first_col + c : first_col + c + 1]
+                nc.tensor.transpose(acc[:, c * P : (c + 1) * P], col.to_broadcast([P, P]), ident16[:])
+
+        def spread_bias(cols):
+            acc = bank(BF16, 2 * BANK)
+            spread(cols, 0, acc)
+            for h in range(2):
+                nc.scalar.copy(
+                    out=bias_bc[:, h * H : (h + 1) * H].rearrange("p (u k e) -> p u k e", u=2, e=2),
+                    in_=acc[:, h * H : (h + 1) * H].rearrange("p (k u e) -> p u k e", u=2, e=2),
+                )
+
+        def spread_gain(cols):
+            for h in range(2):
+                if GP:
+                    acc = psum.tile([P, HALF], BF16, name="gain_acc", tag="gain_acc", bufs=2)
+                    spread(cols, Q // P + h * HALF // P, acc)
+                    gain_of[h] = acc[:]
+                else:
+                    acc = bank(BF16, 2 * BANK)
+                    spread(cols, Q // P + h * HALF // P, acc)
+                    nc.scalar.copy(out=gain_bc[:, h * HALF : (h + 1) * HALF], in_=acc[:])
+                    gain_of[h] = gain_bc[:, h * HALF : (h + 1) * HALF]
+
+        wo_codes = keep.tile([P, Q], U32, name="wo_codes", align_bytes=64)
+        wo_plane = keep.tile([P, Q], U8, name="wo_plane", align_bytes=64)
+        wo_grouped = [keep.tile([P, 4 * H], BF16, name="wo_grouped%d" % h, align_bytes=64) for h in range(2)]
+
+        def group_wo(h):
+            nc.vector.tensor_copy(
+                out=wo_grouped[h][:].rearrange("p (c i j) -> p c j i", i=4, j=4),
+                in_=wo_raw[h][:].rearrange("p j (c i) -> p c j i", i=4),
+            )
+
+        def quantize_wo(h):
+            cols = slice(h * H, (h + 1) * H)
+            nc.vector.quantize_mx(
+                out=wo_codes[:, cols].bitcast(FP8X4), scales=wo_plane[:, cols], in_=wo_grouped[h][:]
+            )
+
+        x_grouped, x_codes, x_plane = {}, {}, {}
+        u_acc, u_sorted, u_grouped, u_codes, u_plane = {}, {}, {}, {}, {}
+        gate1, gate2, y_f32, y_sorted, y_grouped = {}, {}, {}, {}, {}
+        y_codes = keep.tile([P, CHUNKS, T], U32, name="y_codes", align_bytes=64)
+        y_plane = keep.tile([P, CHUNKS, T], U8, name="y_plane", align_bytes=64)
+
+        def copy_words_out(dst, acc):
+            nc.scalar.copy(
+                out=dst.bitcast(F32).rearrange("p (g r u) -> p g r u", g=2, u=2),
+                in_=acc[:].rearrange("p (g u r) -> p g r u", g=2, u=2),
+            )
+
+        def turn_x(i, banks=(0, 1)):
+            if banks[0] == 0:
+                x_grouped[i] = work.tile([P, XG * KP], BF16, name="x_grouped", align_bytes=64)
+            for b in banks:
+                acc = bank()
+                for g in range(2 * b, 2 * b + 2):
+                    if g == 0:
+                        words = xo_sb[i][:].bitcast(F32)
+                    else:
+                        words = xr_sb[i][:, (g - 1) * KP : g * KP].bitcast(F32)
+                    for u in range(2):
+                        slot = 2 * (g % 2) + u
+                        nc.tensor.transpose(acc[:, slot * P : (slot + 1) * P], words[:, u : 2 * P : 2], ident32[:])
+                copy_words_out(x_grouped[i][:, 2 * b * KP : 2 * (b + 1) * KP], acc)
+
+        def quantize_x(i):
+            x_codes[i] = work.tile([P, XG * P], U32, name="x_codes", bufs=3, align_bytes=64)
+            x_plane[i] = work.tile([P, XG * P], U8, name="x_plane", bufs=3, align_bytes=64)
+            nc.vector.quantize_mx(out=x_codes[i][:].bitcast(FP8X4), scales=x_plane[i][:], in_=x_grouped[i][:])
+
+        def project(i, h):
+            acc = psum.tile([P, BANK], F32, name="u_acc", tag="u_acc", bufs=2)
+            u_acc[i, h] = acc
+            cols = slice(h * H, (h + 1) * H)
+            order = list(range(1, XG)) + [0]
+            for g in order:
+                tok = slice(g * P, (g + 1) * P)
+                if g == 0:
+                    rhs, rhs_scale = wo_codes[:, cols].bitcast(FP8X4), wo_plane[:, cols]
+                else:
+                    rhs, rhs_scale = wr_codes[h][:, g - 1, :].bitcast(FP4X4), wr_plane[:, g - 1, cols]
+                nc.tensor.matmul_mx(
+                    out=acc[:],
+                    lhsT=x_codes[i][:, tok].bitcast(FP8X4),
+                    lhsT_scale=x_plane[i][:, tok],
+                    rhs=rhs,
+                    rhs_scale=rhs_scale,
+                    start=(g == order[0]),
+                    stop=(g == order[-1]),
+                )
+
+        def add_bias(i, h):
+            u_sorted[i, h] = work.tile([P, H], BF16, name="u_sorted", bufs=4)
+            nc.vector.tensor_tensor(
+                out=u_sorted[i, h][:].rearrange("p (u k e) -> p u k e", u=2, e=2),
+                in0=u_acc[i, h][:].rearrange("p (k u e) -> p u k e", u=2, e=2),
+                in1=bias_bc[:, h * H : (h + 1) * H].rearrange("p (u k e) -> p u k e", u=2, e=2),
+                op=ALU.add,
+            )
+
+        def turn_u(i):
+            acc = bank()
+            for h in range(2):
+                words = u_sorted[i, h][:].bitcast(F32)
+                for u in range(2):
+                    slot = 2 * h + u
+                    nc.tensor.transpose(acc[:, slot * P : (slot + 1) * P], words[:, u * P : (u + 1) * P], ident32[:])
+            u_grouped[i] = work.tile([P, Q], BF16, name="u_grouped", align_bytes=64)
+            copy_words_out(u_grouped[i][:], acc)
+
+        def quantize_u(i):
+            u_codes[i] = work.tile([P, 2 * P], U32, name="u_codes", align_bytes=64)
+            u_plane[i] = work.tile([P, 2 * P], U8, name="u_plane", align_bytes=64)
+            nc.vector.quantize_mx(out=u_codes[i][:].bitcast(FP8X4), scales=u_plane[i][:], in_=u_grouped[i][:])
+
+        def score(i, h):
+            gate1[i, h] = work.tile([P, HALF], F32, name="gate1", bufs=3)
+            gate2[i, h] = work.tile([P, HALF], F32, name="gate2", bufs=3)
+            for c in range(2 * h, 2 * h + 2):
+                cols = slice(c * BANK, (c + 1) * BANK)
+                for s, gate in enumerate((gate1[i, h], gate2[i, h])):
+                    tok = slice(s * P, (s + 1) * P)
+                    acc = bank()
+                    nc.tensor.matmul_mx(
+                        out=acc[:],
+                        lhsT=u_codes[i][:, tok].bitcast(FP8X4),
+                        lhsT_scale=u_plane[i][:, tok],
+                        rhs=sub_codes[c][:, s, :].bitcast(FP8X4),
+                        rhs_scale=sub_plane[4 * s :, cols],
+                        start=True,
+                        stop=True,
+                    )
+                    nc.scalar.activation(
+                        out=gate[:, (c % 2) * BANK : (c % 2 + 1) * BANK], in_=acc[:], func=ACT.Sigmoid
+                    )
+
+        def multiply_gates(i, h, cols=slice(0, HALF)):
+            nc.vector.tensor_tensor(out=gate1[i, h][:, cols], in0=gate1[i, h][:, cols], in1=gate2[i, h][:, cols], op=ALU.mult)
+
+        def apply_gain(i, h, cols=slice(0, HALF)):
+            if cols.start == 0:
+                y_f32[i, h] = work.tile([P, HALF], F32, name="y_f32", bufs=4)
+            nc.vector.tensor_tensor(out=y_f32[i, h][:, cols], in0=gate1[i, h][:, cols], in1=gain_of[h][:, cols], op=ALU.mult)
+            if (i, h) == (TILES - 1, 1):
+                nc.sync.dma_start(out=out_0[i * P : (i + 1) * P, h * HALF : (h + 1) * HALF][:, cols], in_=y_f32[i, h][:, cols])
+            elif cols.stop == HALF:
+                nc.sync.dma_start(out=out_0[i * P : (i + 1) * P, h * HALF : (h + 1) * HALF], in_=y_f32[i, h][:])
+
+        def round_y(i, h, c, eng):
+            if c == 0:
+                y_sorted[i, h] = work.tile([P, HALF], BF16, name="y_sorted", bufs=4)
+            cols = slice(c * BANK, (c + 1) * BANK)
+            dst = y_sorted[i, h][:, cols].rearrange("p (u k e) -> p u k e", u=2, e=2)
+            src = y_f32[i, h][:, cols].rearrange("p (k u e) -> p u k e", u=2, e=2)
+            if eng == "pool":
+                nc.gpsimd.tensor_scalar(out=dst, in0=src, scalar1=1.0, scalar2=0.0, op0=ALU.mult, op1=ALU.add)
+            elif eng == "act":
+                nc.scalar.copy(out=dst, in_=src)
+            else:
+                nc.vector.tensor_copy(out=dst, in_=src)
+
+        def turn_y(i, h, chunks=(0, 1)):
+            acc = bank()
+            words = y_sorted[i, h][:].bitcast(F32)
+            for c in chunks:
+                for u in range(2):
+                    slot = 2 * c + u
+                    nc.tensor.transpose(acc[:, slot * P : (slot + 1) * P], words[:, slot * P : (slot + 1) * P], ident32[:])
+            if chunks[0] == 0:
+                y_grouped[i, h] = work.tile([P, HALF], BF16, name="y_grouped", bufs=3, align_bytes=64)
+            lo, hi = chunks[0], chunks[-1] + 1
+            nc.scalar.copy(
+                out=y_grouped[i, h][:, lo * KP : hi * KP].bitcast(F32).rearrange("p (g r u) -> p g r u", r=P, u=2),
+                in_=acc[:, lo * 2 * P : hi * 2 * P].rearrange("p (g u r) -> p g r u", r=P, u=2),
+            )
+
+        def quantize_y(i, h, chunks=(0, 1)):
+            tok = slice(i * P, (i + 1) * P)
+            for c in chunks:
+                nc.vector.quantize_mx(
+                    out=y_codes[:, 2 * h + c, tok].bitcast(FP8X4),
+                    scales=y_plane[:, 2 * h + c, tok],
+                    in_=y_grouped[i, h][:, c * KP : (c + 1) * KP],
+                )
+
+        def store_planes(first, last):
+            tok = slice(first * P, last * P)
+            words = out_1.rearrange("g p m t -> p g (m t)").bitcast(I32)
+            nc.sync.dma_start(out=words[:, :, tok], in_=y_codes[:, :, tok].bitcast(I32))
+
+        def store_scales(first, last):
+            tok = slice(first * P, last * P)
+            for q in range(4):
+                nc.sync.dma_start(
+                    out=out_2[:, 4 * q : 4 * q + 4, tok].rearrange("g r m -> r g m").bitcast(I32),
+                    in_=y_plane[32 * q : 32 * q + 4, :, tok].bitcast(I32),
+                )
+
+        def live(i):
+            return 0 <= i < TILES
+
+        def round_half(i, h):
+            for c in range(2):
+                round_y(i, h, c, "pool" if GP else ("act" if (2 * h + c) < ACT_CAST else "dve"))
+
+        def finish(i):
+            quantize_y(i, 1)
+            if i % 2 == 1 and i < TILES - 1:
+                store_planes(i - 1, i + 1)
+            if i == TILES - 3:
+                store_scales(0, TILES - 2)
+            if i == TILES - 2:
+                store_planes(i, i + 1)
+            if i == TILES - 1:
+                store_planes(i, i + 1)
+                store_scales(TILES - 2, TILES)
+
+        def at(lags, s):
+            return [j for j in range(TILES) if 2 * j - lags[j] == s]
+
+        def half(s):
+            return (s // 2, s % 2) if 0 <= s < 2 * TILES else None
+
+        warm = keep.tile([P, 2], F32, name="warm")
+        nc.scalar.activation(out=warm[:], in_=ident32[:, 0:2], func=ACT.Sigmoid)
+        turn_x(0)
+        vec_cols = turn_vector(vec_rows)
+        spread_bias(vec_cols)
+        group_wo(0)
+        quantize_x(0)
+        quantize_wo(0)
+        if SHALLOW:
+            group_wo(1)
+            project(0, 0)
+            quantize_wo(1)
+            project(0, 1)
+            add_bias(0, 0)
+            add_bias(0, 1)
+            turn_x(1, (0,))
+            turn_u(0)
+            turn_x(1, (1,))
+            quantize_u(0)
+            quantize_x(1)
+            if not GDMA:
+                spread_gain(vec_cols)
+        else:
+            project(0, 0)
+            turn_x(1)
+            group_wo(1)
+            quantize_wo(1)
+            add_bias(0, 0)
+            project(0, 1)
+            quantize_x(1)
+            add_bias(0, 1)
+            project(1, 0)
+            turn_u(0)
+            add_bias(1, 0)
+            project(1, 1)
+            quantize_u(0)
+            add_bias(1, 1)
+        for s in range(FIRST, 2 * TILES):
+            if s in S2FIRST and half(s):
+                score(*half(s))
+            for j in at(SA, s):
+                project(j, 0)
+            for j in at(SB, s):
+                project(j, 1)
+            if s not in S2FIRST and half(s):
+                score(*half(s))
+            if half(s - 1):
+                multiply_gates(*half(s - 1))
+            if not POOL:
+                for j in at(SA, s):
+                    add_bias(j, 0)
+                for j in at(SB, s):
+                    add_bias(j, 1)
+            if POOL and half(s - LY - 1):
+                i, h = half(s - LY - 1)
+                if h:
+                    finish(i)
+                else:
+                    quantize_y(i, 0)
+            for j in at(UT, s - 1):
+                if UT[j] > 1:
+                    quantize_u(j)
+            for j in at(XB, s - 1):
+                if XB[j] - SA[j] > 1:
+                    quantize_x(j)
+            on_act = ACT_CAST and (s % ACT_EVERY == 0 or s >= ACT_FROM) and s < 2 * TILES
+            if POOL:
+                if half(s - 1):
+                    for c in range(2):
+                        apply_gain(*half(s - 1), slice(c * BANK, (c + 1) * BANK))
+                        round_y(*half(s - 1), c, "pool")
+                for j in at(SA, s):
+                    add_bias(j, 0)
+                for j in at(SB, s):
+                    add_bias(j, 1)
+            else:
+                if half(s - 1):
+                    apply_gain(*half(s - 1))
+                if half(s - LY - 1):
+                    i, h = half(s - LY - 1)
+                    if h:
+                        finish(i)
+                    else:
+                        quantize_y(i, 0)
+                if half(s - 1):
+                    round_y(*half(s - 1), 0, "dve")
+                    if not on_act:
+                        round_y(*half(s - 1), 1, "dve")
+            for j in at(UT, s):
+                if SB[j] > UT[j]:
+                    turn_u(j)
+            for j in at(XA, s):
+                turn_x(j, (0,))
+            for j in at(XB, s):
+                turn_x(j, (1,))
+            if s == 0 and not GDMA and not SHALLOW:
+                spread_gain(vec_cols)
+            if half(s - LY):
+                turn_y(*half(s - LY))
+            for j in at(UT, s):
+                if SB[j] == UT[j]:
+                    turn_u(j)
+            if half(s - 1) and on_act and not POOL:
+                round_y(*half(s - 1), 1, "act")
+            for j in at(UT, s):
+                if UT[j] == 1:
+                    quantize_u(j)
+            for j in at(XB, s):
+                if XB[j] - SA[j] == 1:
+                    quantize_x(j)
+        last = TILES - 1
+        chunk = [slice(0, BANK), slice(BANK, HALF)]
+        multiply_gates(last, 1, chunk[0])
+        quantize_y(last - 1, 1, (0,))
+        apply_gain(last, 1, chunk[0])
+        turn_y(last, 0)
+        multiply_gates(last, 1, chunk[1])
+        round_y(last, 1, 0, "act")
+        quantize_y(last - 1, 1, (1,))
+        store_planes(last - 1, last)
+        apply_gain(last, 1, chunk[1])
+        turn_y(last, 1, (0,))
+        quantize_y(last, 0)
+        round_y(last, 1, 1, "dve")
+        turn_y(last, 1, (1,))
+        quantize_y(last, 1)
+        store_planes(last, TILES)
+        store_scales(TILES - 2, TILES)

@@ -23,21 +23,28 @@ TILES = T // P
 XG = (DO + DR) // KP
 CHUNKS = N // BANK
 HALF = N // 2
-GP = 0
-ACT_CAST = 1
-XA = [99,99,4,5,6,6,6,6]
-XB = [99,99,4,5,5,5,5,5]
-SA = [99,2,2,3,3,3,3,3]
-SB = [99,2,2,2,2,2,2,2]
-UT = [99,1,2,2,2,2,2,2]
-LY = 2
-ACT_FROM = 15
-GDMA = 1
+GP = 1
+ACT_CAST = 0
+XA = [99,99,4,5,6,7,7,8]
+XB = [99,99,4,5,6,6,7,7]
+SA = [99,99,2,3,3,4,4,5]
+SB = [99,2,2,2,3,3,4,4]
+UT = [99,2,2,2,2,3,3,3]
+LY = 3
+ACT_FROM = 11
+GDMA = 0
 ACT_EVERY = 2
-POOL = 0
+POOL = 1
 SHALLOW = 1
+ROT = 0
+DV = "PXGBYU"
+GSLOT = 0
+TAILENG = "act"
+UB = 2
+GEARLY = 0
+HEAD = 1
 FIRST = 0
-S2FIRST = [0]
+S2FIRST = []
 
 
 def tile_paired_subkey_router_k6_kernel(
@@ -51,7 +58,7 @@ def tile_paired_subkey_router_k6_kernel(
         ctx.enter_context(tc.manual_schedule())
 
         def bank(dtype=F32, width=BANK):
-            return psum.tile([P, width], dtype, name="bank", tag="bank", bufs=4 if GP else 6)
+            return psum.tile([P, width], dtype, name="bank", tag="bank", bufs=(6 if GP else 8) - UB)
 
         ident32 = keep.tile([P, P], F32, name="ident32")
         ident16 = keep.tile([P, P], BF16, name="ident16")
@@ -66,16 +73,16 @@ def tile_paired_subkey_router_k6_kernel(
         xr_sb = [keep.tile([P, DR], BF16, name="xr%d" % i) for i in range(TILES)]
         wo_raw = [keep.tile([P, 4, H], BF16, name="wo_raw%d" % h) for h in range(2)]
         wr_codes = [keep.tile([P, XG - 1, 2 * H], U8, name="wr_codes%d" % h, align_bytes=64) for h in range(2)]
-        sub_codes = [keep.tile([P, 2, BANK], U32, name="sub_codes%d" % c, align_bytes=64) for c in range(CHUNKS)]
+        sub_codes = [keep.tile([P, HALF], U32, name="sub_codes%d" % c, align_bytes=64) for c in range(4)]
 
         def load_x(i):
             rows = slice(i * P, (i + 1) * P)
             nc.sync.dma_start(out=xo_sb[i][:], in_=xo[rows, :])
             nc.sync.dma_start(out=xr_sb[i][:], in_=xr[rows, :])
 
-        def load_sub(c):
-            cols = sub_words.rearrange("g p n t -> p g (n t)")[:, :, 4 * BANK * c : 4 * BANK * (c + 1)]
-            nc.sync.dma_start(out=sub_codes[c][:].bitcast(I32), in_=cols.bitcast(I32))
+        def load_sub(s, h):
+            cols = sub_words[s].rearrange("p n t -> p (n t)")[:, 4 * HALF * h : 4 * HALF * (h + 1)]
+            nc.sync.dma_start(out=sub_codes[2 * s + h][:].bitcast(I32), in_=cols.bitcast(I32))
 
         def load_wo(h):
             nc.sync.dma_start(
@@ -101,24 +108,24 @@ def tile_paired_subkey_router_k6_kernel(
                 out=wr_plane[32 * q : 32 * q + 4, :, :].bitcast(I32),
                 in_=wr_scales[:, 4 * q : 4 * q + 4, :].rearrange("g r n -> r g n").bitcast(I32),
             )
-        if SHALLOW:
-            load_wo(1)
-            load_wr(1)
+        load_wo(1)
+        load_wr(1)
+        if HEAD:
             load_x(1)
-        else:
-            load_x(1)
-            load_wo(1)
-            load_wr(1)
-        load_sub(0)
-        load_sub(1)
+        load_sub(0, 0)
         for q in range(4):
             nc.sync.dma_start(
                 out=sub_plane[32 * q : 32 * q + 8, :].bitcast(I32),
                 in_=sub_scales[:, 4 * q : 4 * q + 4, :].bitcast(I32),
             )
+        if not HEAD:
+            load_x(1)
+            load_sub(0, 1)
+        load_sub(1, 0)
+        if HEAD:
+            load_sub(0, 1)
+        load_sub(1, 1)
         load_x(2)
-        load_sub(2)
-        load_sub(3)
         gain_bc = keep.tile([P, N], BF16, name="gain_bc")
         gain_of = {}
         for i in range(3, TILES):
@@ -182,8 +189,7 @@ def tile_paired_subkey_router_k6_kernel(
         x_grouped, x_codes, x_plane = {}, {}, {}
         u_acc, u_sorted, u_grouped, u_codes, u_plane = {}, {}, {}, {}, {}
         gate1, gate2, y_f32, y_sorted, y_grouped = {}, {}, {}, {}, {}
-        y_codes = keep.tile([P, CHUNKS, T], U32, name="y_codes", align_bytes=64)
-        y_plane = keep.tile([P, CHUNKS, T], U8, name="y_plane", align_bytes=64)
+        y_codes, y_plane, gates = {}, {}, {}
 
         def copy_words_out(dst, acc):
             nc.scalar.copy(
@@ -193,7 +199,7 @@ def tile_paired_subkey_router_k6_kernel(
 
         def turn_x(i, banks=(0, 1)):
             if banks[0] == 0:
-                x_grouped[i] = work.tile([P, XG * KP], BF16, name="x_grouped", align_bytes=64)
+                x_grouped[i] = work.tile([P, XG * KP], BF16, name="x_grouped", bufs=3, align_bytes=64)
             for b in banks:
                 acc = bank()
                 for g in range(2 * b, 2 * b + 2):
@@ -211,26 +217,29 @@ def tile_paired_subkey_router_k6_kernel(
             x_plane[i] = work.tile([P, XG * P], U8, name="x_plane", bufs=3, align_bytes=64)
             nc.vector.quantize_mx(out=x_codes[i][:].bitcast(FP8X4), scales=x_plane[i][:], in_=x_grouped[i][:])
 
-        def project(i, h):
-            acc = psum.tile([P, BANK], F32, name="u_acc", tag="u_acc", bufs=2)
-            u_acc[i, h] = acc
+        def project_pass(i, h, n):
+            if n == 0:
+                u_acc[i, h] = psum.tile([P, BANK], F32, name="u_acc", tag="u_acc", bufs=UB)
+            g = (n + 1) % XG
+            tok = slice(g * P, (g + 1) * P)
             cols = slice(h * H, (h + 1) * H)
-            order = list(range(1, XG)) + [0]
-            for g in order:
-                tok = slice(g * P, (g + 1) * P)
-                if g == 0:
-                    rhs, rhs_scale = wo_codes[:, cols].bitcast(FP8X4), wo_plane[:, cols]
-                else:
-                    rhs, rhs_scale = wr_codes[h][:, g - 1, :].bitcast(FP4X4), wr_plane[:, g - 1, cols]
-                nc.tensor.matmul_mx(
-                    out=acc[:],
-                    lhsT=x_codes[i][:, tok].bitcast(FP8X4),
-                    lhsT_scale=x_plane[i][:, tok],
-                    rhs=rhs,
-                    rhs_scale=rhs_scale,
-                    start=(g == order[0]),
-                    stop=(g == order[-1]),
-                )
+            if g == 0:
+                rhs, rhs_scale = wo_codes[:, cols].bitcast(FP8X4), wo_plane[:, cols]
+            else:
+                rhs, rhs_scale = wr_codes[h][:, g - 1, :].bitcast(FP4X4), wr_plane[:, g - 1, cols]
+            nc.tensor.matmul_mx(
+                out=u_acc[i, h][:],
+                lhsT=x_codes[i][:, tok].bitcast(FP8X4),
+                lhsT_scale=x_plane[i][:, tok],
+                rhs=rhs,
+                rhs_scale=rhs_scale,
+                start=(n == 0),
+                stop=(n == XG - 1),
+            )
+
+        def project(i, h):
+            for n in range(XG):
+                project_pass(i, h, n)
 
         def add_bias(i, h):
             u_sorted[i, h] = work.tile([P, H], BF16, name="u_sorted", bufs=4)
@@ -241,41 +250,56 @@ def tile_paired_subkey_router_k6_kernel(
                 op=ALU.add,
             )
 
-        def turn_u(i):
+        def turn_u(i, halves=(0, 1)):
             acc = bank()
-            for h in range(2):
+            for h in halves:
                 words = u_sorted[i, h][:].bitcast(F32)
                 for u in range(2):
                     slot = 2 * h + u
                     nc.tensor.transpose(acc[:, slot * P : (slot + 1) * P], words[:, u * P : (u + 1) * P], ident32[:])
-            u_grouped[i] = work.tile([P, Q], BF16, name="u_grouped", align_bytes=64)
-            copy_words_out(u_grouped[i][:], acc)
+            if halves[0] == 0:
+                u_grouped[i] = work.tile([P, Q], BF16, name="u_grouped", align_bytes=64)
+            lo, hi = halves[0], halves[-1] + 1
+            nc.scalar.copy(
+                out=u_grouped[i][:, lo * KP : hi * KP].bitcast(F32).rearrange("p (g r u) -> p g r u", r=P, u=2),
+                in_=acc[:, lo * 2 * P : hi * 2 * P].rearrange("p (g u r) -> p g r u", r=P, u=2),
+            )
 
-        def quantize_u(i):
-            u_codes[i] = work.tile([P, 2 * P], U32, name="u_codes", align_bytes=64)
-            u_plane[i] = work.tile([P, 2 * P], U8, name="u_plane", align_bytes=64)
-            nc.vector.quantize_mx(out=u_codes[i][:].bitcast(FP8X4), scales=u_plane[i][:], in_=u_grouped[i][:])
+        def quantize_u(i, halves=(0, 1)):
+            if halves[0] == 0:
+                u_codes[i] = work.tile([P, 2 * P], U32, name="u_codes", bufs=3, align_bytes=64)
+                u_plane[i] = work.tile([P, 2 * P], U8, name="u_plane", bufs=3, align_bytes=64)
+            lo, hi = halves[0], halves[-1] + 1
+            nc.vector.quantize_mx(
+                out=u_codes[i][:, lo * P : hi * P].bitcast(FP8X4),
+                scales=u_plane[i][:, lo * P : hi * P],
+                in_=u_grouped[i][:, lo * KP : hi * KP],
+            )
+
+        def gate(i, h, c, s):
+            if (i, h, s) not in gates:
+                gates[i, h, s] = work.tile([P, HALF], F32, name="gate%d" % s, bufs=3 + 2 * s)
+                (gate1, gate2)[s][i, h] = gates[i, h, s]
+            tok = slice(s * P, (s + 1) * P)
+            cols = slice(c * BANK, (c + 1) * BANK)
+            acc = bank()
+            nc.tensor.matmul_mx(
+                out=acc[:],
+                lhsT=u_codes[i][:, tok].bitcast(FP8X4),
+                lhsT_scale=u_plane[i][:, tok],
+                rhs=sub_codes[2 * s + h][:, cols].bitcast(FP8X4),
+                rhs_scale=sub_plane[4 * s :, h * HALF + c * BANK : h * HALF + (c + 1) * BANK],
+                start=True,
+                stop=True,
+            )
+            nc.scalar.activation(out=gates[i, h, s][:, cols], in_=acc[:], func=ACT.Sigmoid)
 
         def score(i, h):
-            gate1[i, h] = work.tile([P, HALF], F32, name="gate1", bufs=3)
-            gate2[i, h] = work.tile([P, HALF], F32, name="gate2", bufs=3)
-            for c in range(2 * h, 2 * h + 2):
-                cols = slice(c * BANK, (c + 1) * BANK)
-                for s, gate in enumerate((gate1[i, h], gate2[i, h])):
-                    tok = slice(s * P, (s + 1) * P)
-                    acc = bank()
-                    nc.tensor.matmul_mx(
-                        out=acc[:],
-                        lhsT=u_codes[i][:, tok].bitcast(FP8X4),
-                        lhsT_scale=u_plane[i][:, tok],
-                        rhs=sub_codes[c][:, s, :].bitcast(FP8X4),
-                        rhs_scale=sub_plane[4 * s :, cols],
-                        start=True,
-                        stop=True,
-                    )
-                    nc.scalar.activation(
-                        out=gate[:, (c % 2) * BANK : (c % 2 + 1) * BANK], in_=acc[:], func=ACT.Sigmoid
-                    )
+            if i == 0:
+                return
+            for c in range(2):
+                for s in range(2):
+                    gate(i, h, c, s)
 
         def multiply_gates(i, h, cols=slice(0, HALF)):
             nc.vector.tensor_tensor(out=gate1[i, h][:, cols], in0=gate1[i, h][:, cols], in1=gate2[i, h][:, cols], op=ALU.mult)
@@ -289,12 +313,16 @@ def tile_paired_subkey_router_k6_kernel(
             elif cols.stop == HALF:
                 nc.sync.dma_start(out=out_0[i * P : (i + 1) * P, h * HALF : (h + 1) * HALF], in_=y_f32[i, h][:])
 
-        def round_y(i, h, c, eng):
-            if c == 0:
-                y_sorted[i, h] = work.tile([P, HALF], BF16, name="y_sorted", bufs=4)
-            cols = slice(c * BANK, (c + 1) * BANK)
-            dst = y_sorted[i, h][:, cols].rearrange("p (u k e) -> p u k e", u=2, e=2)
-            src = y_f32[i, h][:, cols].rearrange("p (k u e) -> p u k e", u=2, e=2)
+        def round_y(i, h, chunks, eng, into=None):
+            if chunks[0] == 0:
+                if into is None:
+                    own = work.tile([P, HALF], BF16, name="y_sorted", bufs=3)
+                    y_sorted[i, h] = own[:]
+                else:
+                    y_sorted[i, h] = into[:].bitcast(BF16)[:, 0:HALF]
+            ks = slice(chunks[0] * P, (chunks[-1] + 1) * P)
+            dst = y_sorted[i, h].rearrange("p (u k e) -> p u k e", u=2, e=2)[:, :, ks, :]
+            src = y_f32[i, h][:].rearrange("p (k u e) -> p u k e", u=2, e=2)[:, :, ks, :]
             if eng == "pool":
                 nc.gpsimd.tensor_scalar(out=dst, in0=src, scalar1=1.0, scalar2=0.0, op0=ALU.mult, op1=ALU.add)
             elif eng == "act":
@@ -304,59 +332,54 @@ def tile_paired_subkey_router_k6_kernel(
 
         def turn_y(i, h, chunks=(0, 1)):
             acc = bank()
-            words = y_sorted[i, h][:].bitcast(F32)
+            words = y_sorted[i, h].bitcast(F32)
             for c in chunks:
                 for u in range(2):
                     slot = 2 * c + u
-                    nc.tensor.transpose(acc[:, slot * P : (slot + 1) * P], words[:, slot * P : (slot + 1) * P], ident32[:])
-            if chunks[0] == 0:
-                y_grouped[i, h] = work.tile([P, HALF], BF16, name="y_grouped", bufs=3, align_bytes=64)
+                    first = (2 * u + c) * P
+                    nc.tensor.transpose(acc[:, slot * P : (slot + 1) * P], words[:, first : first + P], ident32[:])
+            if chunks[0] == 0 and i % 2 == 0:
+                y_grouped[i // 2, h] = work.tile([P, 2, 2 * KP], BF16, name="y_grouped", bufs=3, align_bytes=64)
             lo, hi = chunks[0], chunks[-1] + 1
             nc.scalar.copy(
-                out=y_grouped[i, h][:, lo * KP : hi * KP].bitcast(F32).rearrange("p (g r u) -> p g r u", r=P, u=2),
+                out=y_grouped[i // 2, h][:, lo:hi, (i % 2) * KP : (i % 2 + 1) * KP].bitcast(F32).rearrange("p g (r u) -> p g r u", u=2),
                 in_=acc[:, lo * 2 * P : hi * 2 * P].rearrange("p (g u r) -> p g r u", r=P, u=2),
             )
 
-        def quantize_y(i, h, chunks=(0, 1)):
-            tok = slice(i * P, (i + 1) * P)
-            for c in chunks:
-                nc.vector.quantize_mx(
-                    out=y_codes[:, 2 * h + c, tok].bitcast(FP8X4),
-                    scales=y_plane[:, 2 * h + c, tok],
-                    in_=y_grouped[i, h][:, c * KP : (c + 1) * KP],
-                )
+        def quantize_y(pair, h, c, tiles=(0, 1)):
+            if pair not in y_codes:
+                y_codes[pair] = work.tile([P, CHUNKS, 2 * P], U32, name="y_codes", align_bytes=64)
+                y_plane[pair] = work.tile([P, CHUNKS, 2 * P], U8, name="y_plane", align_bytes=64)
+            lo, hi = tiles[0], tiles[-1] + 1
+            nc.vector.quantize_mx(
+                out=y_codes[pair][:, 2 * h + c, lo * P : hi * P].bitcast(FP8X4),
+                scales=y_plane[pair][:, 2 * h + c, lo * P : hi * P],
+                in_=y_grouped[pair, h][:, c, lo * KP : hi * KP],
+            )
 
-        def store_planes(first, last):
-            tok = slice(first * P, last * P)
+        def store_words(pair, lo, hi):
+            tok = slice(2 * pair * P, 2 * (pair + 1) * P)
             words = out_1.rearrange("g p m t -> p g (m t)").bitcast(I32)
-            nc.sync.dma_start(out=words[:, :, tok], in_=y_codes[:, :, tok].bitcast(I32))
+            nc.sync.dma_start(out=words[:, lo:hi, tok], in_=y_codes[pair][:, lo:hi, :].bitcast(I32))
 
-        def store_scales(first, last):
-            tok = slice(first * P, last * P)
+        def store_scales(pair, queues):
+            tok = slice(2 * pair * P, 2 * (pair + 1) * P)
             for q in range(4):
-                nc.sync.dma_start(
+                queues[q % len(queues)].dma_start(
                     out=out_2[:, 4 * q : 4 * q + 4, tok].rearrange("g r m -> r g m").bitcast(I32),
-                    in_=y_plane[32 * q : 32 * q + 4, :, tok].bitcast(I32),
+                    in_=y_plane[pair][32 * q : 32 * q + 4, :, :].bitcast(I32),
                 )
 
         def live(i):
             return 0 <= i < TILES
 
-        def round_half(i, h):
-            for c in range(2):
-                round_y(i, h, c, "pool" if GP else ("act" if (2 * h + c) < ACT_CAST else "dve"))
-
-        def finish(i):
-            quantize_y(i, 1)
-            if i % 2 == 1 and i < TILES - 1:
-                store_planes(i - 1, i + 1)
-            if i == TILES - 3:
-                store_scales(0, TILES - 2)
-            if i == TILES - 2:
-                store_planes(i, i + 1)
-            if i == TILES - 1:
-                store_planes(i, i + 1)
-                store_scales(TILES - 2, TILES)
+        def finish(i, h):
+            if i % 2:
+                quantize_y(i // 2, h, 0)
+                quantize_y(i // 2, h, 1)
+                if h:
+                    store_words(i // 2, 0, CHUNKS)
+                    store_scales(i // 2, [nc.sync])
 
         def at(lags, s):
             return [j for j in range(TILES) if 2 * j - lags[j] == s]
@@ -369,89 +392,108 @@ def tile_paired_subkey_router_k6_kernel(
         turn_x(0)
         vec_cols = turn_vector(vec_rows)
         spread_bias(vec_cols)
+        if GEARLY:
+            spread_gain(vec_cols)
         group_wo(0)
         quantize_x(0)
         quantize_wo(0)
-        if SHALLOW:
-            group_wo(1)
-            project(0, 0)
-            quantize_wo(1)
-            project(0, 1)
-            add_bias(0, 0)
+        group_wo(1)
+        project(0, 0)
+        quantize_wo(1)
+        project(0, 1)
+        add_bias(0, 0)
+        if HEAD == 0:
+            turn_u(0, (0,))
             add_bias(0, 1)
-            turn_x(1, (0,))
-            turn_u(0)
-            turn_x(1, (1,))
-            quantize_u(0)
-            quantize_x(1)
-            if not GDMA:
-                spread_gain(vec_cols)
-        else:
-            project(0, 0)
+            quantize_u(0, (0,))
+            turn_u(0, (1,))
+            gate(0, 0, 0, 0)
+            gate(0, 0, 1, 0)
+            quantize_u(0, (1,))
             turn_x(1)
-            group_wo(1)
-            quantize_wo(1)
-            add_bias(0, 0)
-            project(0, 1)
             quantize_x(1)
-            add_bias(0, 1)
+            gate(0, 1, 0, 0)
+            gate(0, 1, 1, 0)
+            gate(0, 0, 0, 1)
+            gate(0, 0, 1, 1)
+            if not GEARLY:
+                spread_gain(vec_cols)
             project(1, 0)
-            turn_u(0)
             add_bias(1, 0)
-            project(1, 1)
-            quantize_u(0)
-            add_bias(1, 1)
-        for s in range(FIRST, 2 * TILES):
-            if s in S2FIRST and half(s):
-                score(*half(s))
-            for j in at(SA, s):
-                project(j, 0)
-            for j in at(SB, s):
-                project(j, 1)
-            if s not in S2FIRST and half(s):
-                score(*half(s))
-            if half(s - 1):
-                multiply_gates(*half(s - 1))
-            if not POOL:
-                for j in at(SA, s):
-                    add_bias(j, 0)
-                for j in at(SB, s):
-                    add_bias(j, 1)
-            if POOL and half(s - LY - 1):
-                i, h = half(s - LY - 1)
-                if h:
-                    finish(i)
-                else:
-                    quantize_y(i, 0)
-            for j in at(UT, s - 1):
-                if UT[j] > 1:
-                    quantize_u(j)
-            for j in at(XB, s - 1):
-                if XB[j] - SA[j] > 1:
-                    quantize_x(j)
-            on_act = ACT_CAST and (s % ACT_EVERY == 0 or s >= ACT_FROM) and s < 2 * TILES
+            gate(0, 1, 0, 1)
+            gate(0, 1, 1, 1)
+        else:
+            turn_u(0, (0,))
+            add_bias(0, 1)
+            quantize_u(0, (0,))
+            turn_x(1, (0,))
+            turn_u(0, (1,))
+            turn_x(1, (1,))
+            quantize_u(0, (1,))
+            quantize_x(1)
+            gate(0, 0, 0, 0)
+            gate(0, 0, 1, 0)
+            gate(0, 0, 0, 1)
+            gate(0, 0, 1, 1)
+            if not GEARLY:
+                spread_gain(vec_cols)
+            for n in range(4):
+                project_pass(1, 0, n)
+                gate(0, 1, n // 2, n % 2)
+            add_bias(1, 0)
+        for s in range(FIRST, 2 * TILES - 1):
+            todo = [(j, 0, n) for j in at(SA, s) for n in range(XG)] + [(j, 1, n) for j in at(SB, s) for n in range(XG)]
+            per = len(todo) // 4
+            for n in range(4):
+                if s in S2FIRST and s > 1:
+                    gate(*half(s), n // 2, n % 2)
+                for job in todo[n * per : (n + 1) * per]:
+                    project_pass(*job)
+                if s not in S2FIRST and s > 1:
+                    gate(*half(s), n // 2, n % 2)
             if POOL:
+                for step in DV:
+                    if step == "Y" and half(s - LY - 1):
+                        finish(*half(s - LY - 1))
+                    if step == "U":
+                        for j in at(UT, s - 1):
+                            if UT[j] > 1:
+                                quantize_u(j)
+                    if step == "X":
+                        for j in at(XB, s - 1):
+                            if XB[j] - SA[j] > 1:
+                                quantize_x(j)
+                    if step == "P" and half(s - 1):
+                        multiply_gates(*half(s - 1))
+                        if half(s - 2):
+                            round_y(*half(s - 2), (0, 1), "pool", gate2[half(s - 1)])
+                    if step == "B":
+                        for j in at(SA, s):
+                            add_bias(j, 0)
+                        for j in at(SB, s):
+                            add_bias(j, 1)
+                    if step == "G" and half(s - 1):
+                        apply_gain(*half(s - 1))
+            else:
                 if half(s - 1):
-                    for c in range(2):
-                        apply_gain(*half(s - 1), slice(c * BANK, (c + 1) * BANK))
-                        round_y(*half(s - 1), c, "pool")
+                    multiply_gates(*half(s - 1))
                 for j in at(SA, s):
                     add_bias(j, 0)
                 for j in at(SB, s):
                     add_bias(j, 1)
-            else:
+                for j in at(UT, s - 1):
+                    if UT[j] > 1:
+                        quantize_u(j)
+                for j in at(XB, s - 1):
+                    if XB[j] - SA[j] > 1:
+                        quantize_x(j)
+                on_act = ACT_CAST and (s % ACT_EVERY == 0 or s >= ACT_FROM)
                 if half(s - 1):
                     apply_gain(*half(s - 1))
                 if half(s - LY - 1):
-                    i, h = half(s - LY - 1)
-                    if h:
-                        finish(i)
-                    else:
-                        quantize_y(i, 0)
+                    finish(*half(s - LY - 1))
                 if half(s - 1):
-                    round_y(*half(s - 1), 0, "dve")
-                    if not on_act:
-                        round_y(*half(s - 1), 1, "dve")
+                    round_y(*half(s - 1), (0,) if on_act else (0, 1), "dve")
             for j in at(UT, s):
                 if SB[j] > UT[j]:
                     turn_u(j)
@@ -459,15 +501,15 @@ def tile_paired_subkey_router_k6_kernel(
                 turn_x(j, (0,))
             for j in at(XB, s):
                 turn_x(j, (1,))
-            if s == 0 and not GDMA and not SHALLOW:
+            if s == GSLOT and not GDMA and not SHALLOW:
                 spread_gain(vec_cols)
             if half(s - LY):
                 turn_y(*half(s - LY))
             for j in at(UT, s):
                 if SB[j] == UT[j]:
                     turn_u(j)
-            if half(s - 1) and on_act and not POOL:
-                round_y(*half(s - 1), 1, "act")
+            if not POOL and half(s - 1) and on_act:
+                round_y(*half(s - 1), (1,), "act")
             for j in at(UT, s):
                 if UT[j] == 1:
                     quantize_u(j)
@@ -476,19 +518,30 @@ def tile_paired_subkey_router_k6_kernel(
                     quantize_x(j)
         last = TILES - 1
         chunk = [slice(0, BANK), slice(BANK, HALF)]
+        score(last, 1)
+        multiply_gates(last, 0)
+        round_y(last - 1, 1, (0, 1), "pool", gate2[last, 0])
+        turn_y(last - 1, 0)
+        apply_gain(last, 0)
         multiply_gates(last, 1, chunk[0])
-        quantize_y(last - 1, 1, (0,))
+        round_y(last, 0, (0, 1), "act")
+        turn_y(last - 1, 1)
+        quantize_y(last // 2 - 1, 1, 0)
         apply_gain(last, 1, chunk[0])
-        turn_y(last, 0)
         multiply_gates(last, 1, chunk[1])
-        round_y(last, 1, 0, "act")
-        quantize_y(last - 1, 1, (1,))
-        store_planes(last - 1, last)
+        round_y(last, 1, (0,), "act")
+        quantize_y(last // 2 - 1, 1, 1)
+        store_words(last // 2 - 1, 0, CHUNKS)
+        store_scales(last // 2 - 1, [nc.sync])
         apply_gain(last, 1, chunk[1])
+        turn_y(last, 0)
         turn_y(last, 1, (0,))
-        quantize_y(last, 0)
-        round_y(last, 1, 1, "dve")
+        round_y(last, 1, (1,), "dve")
         turn_y(last, 1, (1,))
-        quantize_y(last, 1)
-        store_planes(last, TILES)
-        store_scales(TILES - 2, TILES)
+        quantize_y(last // 2, 0, 0)
+        quantize_y(last // 2, 0, 1)
+        store_words(last // 2, 0, 2)
+        quantize_y(last // 2, 1, 0)
+        quantize_y(last // 2, 1, 1)
+        store_words(last // 2, 2, 4)
+        store_scales(last // 2, [nc.scalar, nc.sync])

@@ -17,34 +17,19 @@ ALU = mybir.AluOpType
 ACT = mybir.ActivationFunctionType
 
 P = 128
-KP = 512
+GROUP = 512
 BANK = 512
 TILES = T // P
-XG = (DO + DR) // KP
-CHUNKS = N // BANK
+X_GROUPS = (DO + DR) // GROUP
+E_GROUPS = N // GROUP
 HALF = N // 2
-GP = 1
-ACT_CAST = 0
-XA = [99,99,4,5,6,7,7,8]
-XB = [99,99,4,5,6,6,7,7]
-SA = [99,99,2,3,3,4,4,5]
-SB = [99,2,2,2,3,3,4,4]
-UT = [99,2,2,2,2,3,3,3]
-LY = 3
-ACT_FROM = 11
-GDMA = 0
-ACT_EVERY = 2
-POOL = 1
-SHALLOW = 1
-ROT = 0
-DV = "PXGBYU"
-GSLOT = 0
-TAILENG = "act"
-UB = 2
-GEARLY = 0
-HEAD = 1
-FIRST = 0
-S2FIRST = []
+STEPS = 2 * TILES
+CHUNKS = (slice(0, BANK), slice(BANK, HALF))
+
+TURN_X_AHEAD = (7, 6)
+PROJECT_AHEAD = (4, 3)
+TURN_U_AHEAD = 2
+TURN_Y_BEHIND = 3
 
 
 def tile_paired_subkey_router_k6_kernel(
@@ -57,491 +42,386 @@ def tile_paired_subkey_router_k6_kernel(
         psum = ctx.enter_context(tc.psum_pool(name="psum", bufs=1))
         ctx.enter_context(tc.manual_schedule())
 
-        def bank(dtype=F32, width=BANK):
-            return psum.tile([P, width], dtype, name="bank", tag="bank", bufs=(6 if GP else 8) - UB)
+        def next_bank():
+            return psum.tile([P, BANK], F32, name="bank", tag="bank", bufs=4)
 
-        ident32 = keep.tile([P, P], F32, name="ident32")
-        ident16 = keep.tile([P, P], BF16, name="ident16")
-        vec_rows = keep.tile([P, P], BF16, name="vec_rows")
-        wr_plane = keep.tile([P, XG - 1, Q], U8, name="wr_plane", align_bytes=64)
+        wr_plane = keep.tile([P, X_GROUPS - 1, Q], U8, name="wr_plane", align_bytes=64)
         sub_plane = keep.tile([P, N], U8, name="sub_plane", align_bytes=64)
-        nc.gpsimd.memset(vec_rows[:], 0.0)
         nc.vector.memset(wr_plane[:].rearrange("p g n -> p (g n)").bitcast(I32), 0)
         nc.vector.memset(sub_plane[:].bitcast(I32), 0)
 
+        ident = keep.tile([P, P], F32, name="ident")
+        make_identity(nc, ident[:])
+        bias_rows = keep.tile([P, 8], BF16, name="bias_rows")
+        gain_rows = keep.tile([P, 2, 8], BF16, name="gain_rows")
+        nc.gpsimd.dma_start(out=bias_rows[:], in_=bq.rearrange("(n j) -> n j", j=8))
+        nc.gpsimd.dma_start(out=gain_rows[:], in_=gain.rearrange("(h n j) -> n h j", h=2, j=8))
+
         xo_sb = [keep.tile([P, DO], BF16, name="xo%d" % i) for i in range(TILES)]
         xr_sb = [keep.tile([P, DR], BF16, name="xr%d" % i) for i in range(TILES)]
-        wo_raw = [keep.tile([P, 4, H], BF16, name="wo_raw%d" % h) for h in range(2)]
-        wr_codes = [keep.tile([P, XG - 1, 2 * H], U8, name="wr_codes%d" % h, align_bytes=64) for h in range(2)]
-        sub_codes = [keep.tile([P, HALF], U32, name="sub_codes%d" % c, align_bytes=64) for c in range(4)]
+        wo_raw = [keep.tile([P, 4, H], BF16, name="wo_raw%d" % f) for f in range(2)]
+        wr_codes = [keep.tile([P, X_GROUPS - 1, 2 * H], U8, name="wr_codes%d" % f, align_bytes=64) for f in range(2)]
+        sub_codes = {}
+        for s in range(2):
+            for h in range(2):
+                sub_codes[s, h] = keep.tile([P, HALF], U32, name="sub_codes%d%d" % (s, h), align_bytes=64)
 
         def load_x(i):
             rows = slice(i * P, (i + 1) * P)
             nc.sync.dma_start(out=xo_sb[i][:], in_=xo[rows, :])
             nc.sync.dma_start(out=xr_sb[i][:], in_=xr[rows, :])
 
+        def load_w(f):
+            nc.sync.dma_start(out=wo_raw[f][:], in_=wo[:, f * H : (f + 1) * H].rearrange("(p j) n -> p j n", j=4))
+            nc.sync.dma_start(
+                out=wr_codes[f][:].bitcast(I32),
+                in_=wr_words[:, :, 2 * H * f : 2 * H * (f + 1)].rearrange("g p b -> p g b").bitcast(I32),
+            )
+
         def load_sub(s, h):
             cols = sub_words[s].rearrange("p n t -> p (n t)")[:, 4 * HALF * h : 4 * HALF * (h + 1)]
-            nc.sync.dma_start(out=sub_codes[2 * s + h][:].bitcast(I32), in_=cols.bitcast(I32))
+            nc.sync.dma_start(out=sub_codes[s, h][:].bitcast(I32), in_=cols.bitcast(I32))
 
-        def load_wo(h):
-            nc.sync.dma_start(
-                out=wo_raw[h][:], in_=wo[:, h * H : (h + 1) * H].rearrange("(p j) n -> p j n", j=4)
-            )
-
-        def load_wr(h):
-            nc.sync.dma_start(
-                out=wr_codes[h][:].bitcast(I32),
-                in_=wr_words[:, :, 2 * H * h : 2 * H * (h + 1)].rearrange("g p b -> p g b").bitcast(I32),
-            )
-
-        nc.gpsimd.dma_start(out=vec_rows[0 : Q // P, :], in_=bq.rearrange("(c p) -> c p", p=P))
-        if not GDMA:
-            nc.gpsimd.dma_start(out=vec_rows[Q // P : (Q + N) // P, :], in_=gain.rearrange("(c p) -> c p", p=P))
-        make_identity(nc, ident32[:])
-        make_identity(nc, ident16[:])
         load_x(0)
-        load_wo(0)
-        load_wr(0)
-        for q in range(4):
+        load_w(0)
+        for quad in range(4):
             nc.sync.dma_start(
-                out=wr_plane[32 * q : 32 * q + 4, :, :].bitcast(I32),
-                in_=wr_scales[:, 4 * q : 4 * q + 4, :].rearrange("g r n -> r g n").bitcast(I32),
+                out=wr_plane[32 * quad : 32 * quad + 4, :, :].bitcast(I32),
+                in_=wr_scales[:, 4 * quad : 4 * quad + 4, :].rearrange("g r n -> r g n").bitcast(I32),
             )
-        load_wo(1)
-        load_wr(1)
-        if HEAD:
-            load_x(1)
+        load_w(1)
+        load_x(1)
         load_sub(0, 0)
-        for q in range(4):
+        for quad in range(4):
             nc.sync.dma_start(
-                out=sub_plane[32 * q : 32 * q + 8, :].bitcast(I32),
-                in_=sub_scales[:, 4 * q : 4 * q + 4, :].bitcast(I32),
+                out=sub_plane[32 * quad : 32 * quad + 8, :].bitcast(I32),
+                in_=sub_scales[:, 4 * quad : 4 * quad + 4, :].bitcast(I32),
             )
-        if not HEAD:
-            load_x(1)
-            load_sub(0, 1)
         load_sub(1, 0)
-        if HEAD:
-            load_sub(0, 1)
+        load_sub(0, 1)
         load_sub(1, 1)
-        load_x(2)
-        gain_bc = keep.tile([P, N], BF16, name="gain_bc")
-        gain_of = {}
-        for i in range(3, TILES):
+        for i in range(2, TILES):
             load_x(i)
-            if i == 3 and GDMA:
-                nc.sync.dma_start(out=gain_bc[:], in_=gain.partition_broadcast(P))
-                for h in range(2):
-                    gain_of[h] = gain_bc[:, h * HALF : (h + 1) * HALF]
 
-        bias_bc = keep.tile([P, Q], BF16, name="bias_bc")
+        bias_sorted = keep.tile([P, Q], BF16, name="bias_sorted")
+        gain_psum = []
 
-        def turn_vector(rows):
-            acc = bank(BF16, 2 * BANK)
-            nc.tensor.transpose(acc[:, 0:P], rows[:], ident16[:])
-            cols = work.tile([P, P], BF16, name="vec_cols")
-            nc.scalar.copy(out=cols[:], in_=acc[:, 0:P])
-            return cols
+        def spread(rows, acc):
+            words = rows.bitcast(F32)
+            for j in range(4):
+                nc.tensor.transpose(acc[:, j * P : (j + 1) * P], words[:, j : j + 1].to_broadcast([P, P]), ident[:])
 
-        def spread(cols, first_col, acc):
-            for c in range(2 * BANK // P):
-                col = cols[:, first_col + c : first_col + c + 1]
-                nc.tensor.transpose(acc[:, c * P : (c + 1) * P], col.to_broadcast([P, P]), ident16[:])
-
-        def spread_bias(cols):
-            acc = bank(BF16, 2 * BANK)
-            spread(cols, 0, acc)
-            for h in range(2):
+        def spread_bias():
+            acc = next_bank()
+            spread(bias_rows[:], acc)
+            for f in range(2):
                 nc.scalar.copy(
-                    out=bias_bc[:, h * H : (h + 1) * H].rearrange("p (u k e) -> p u k e", u=2, e=2),
-                    in_=acc[:, h * H : (h + 1) * H].rearrange("p (k u e) -> p u k e", u=2, e=2),
+                    out=bias_sorted[:, f * H : (f + 1) * H].bitcast(F32).rearrange("p (u n a) -> p u n a", u=2, a=2),
+                    in_=acc[:].rearrange("p (a u n) -> p u n a", a=2, u=2)[:, :, f * P // 2 : (f + 1) * P // 2, :],
                 )
 
-        def spread_gain(cols):
+        def spread_gain():
             for h in range(2):
-                if GP:
-                    acc = psum.tile([P, HALF], BF16, name="gain_acc", tag="gain_acc", bufs=2)
-                    spread(cols, Q // P + h * HALF // P, acc)
-                    gain_of[h] = acc[:]
-                else:
-                    acc = bank(BF16, 2 * BANK)
-                    spread(cols, Q // P + h * HALF // P, acc)
-                    nc.scalar.copy(out=gain_bc[:, h * HALF : (h + 1) * HALF], in_=acc[:])
-                    gain_of[h] = gain_bc[:, h * HALF : (h + 1) * HALF]
+                acc = psum.tile([P, BANK], F32, name="gain_acc", tag="gain_acc", bufs=2)
+                spread(gain_rows[:, h, :], acc)
+                gain_psum.append(acc[:].bitcast(BF16).rearrange("p (j n e) -> p n j e", j=4, e=2))
 
         wo_codes = keep.tile([P, Q], U32, name="wo_codes", align_bytes=64)
         wo_plane = keep.tile([P, Q], U8, name="wo_plane", align_bytes=64)
-        wo_grouped = [keep.tile([P, 4 * H], BF16, name="wo_grouped%d" % h, align_bytes=64) for h in range(2)]
+        wo_grouped = [keep.tile([P, 4 * H], BF16, name="wo_grouped%d" % f, align_bytes=64) for f in range(2)]
 
-        def group_wo(h):
+        def group_wo(f):
             nc.vector.tensor_copy(
-                out=wo_grouped[h][:].rearrange("p (c i j) -> p c j i", i=4, j=4),
-                in_=wo_raw[h][:].rearrange("p j (c i) -> p c j i", i=4),
+                out=wo_grouped[f][:].rearrange("p (c i j) -> p c j i", i=4, j=4),
+                in_=wo_raw[f][:].rearrange("p j (c i) -> p c j i", i=4),
             )
 
-        def quantize_wo(h):
-            cols = slice(h * H, (h + 1) * H)
-            nc.vector.quantize_mx(
-                out=wo_codes[:, cols].bitcast(FP8X4), scales=wo_plane[:, cols], in_=wo_grouped[h][:]
-            )
+        def quantize_wo(f):
+            cols = slice(f * H, (f + 1) * H)
+            nc.vector.quantize_mx(out=wo_codes[:, cols].bitcast(FP8X4), scales=wo_plane[:, cols], in_=wo_grouped[f][:])
 
         x_grouped, x_codes, x_plane = {}, {}, {}
         u_acc, u_sorted, u_grouped, u_codes, u_plane = {}, {}, {}, {}, {}
-        gate1, gate2, y_f32, y_sorted, y_grouped = {}, {}, {}, {}, {}
-        y_codes, y_plane, gates = {}, {}, {}
+        gates, y_f32, y_sorted, y_grouped, y_codes = {}, {}, {}, {}, {}
+        y_plane = keep.tile([P, E_GROUPS, T], U8, name="y_plane", align_bytes=64)
 
-        def copy_words_out(dst, acc):
-            nc.scalar.copy(
-                out=dst.bitcast(F32).rearrange("p (g r u) -> p g r u", g=2, u=2),
-                in_=acc[:].rearrange("p (g u r) -> p g r u", g=2, u=2),
-            )
+        def words_out(copy, dst, acc, first, count):
+            copy(out=dst, in_=acc[:, first * 2 * P : (first + count) * 2 * P].rearrange("p (g u r) -> p g r u", r=P, u=2))
 
-        def turn_x(i, banks=(0, 1)):
-            if banks[0] == 0:
-                x_grouped[i] = work.tile([P, XG * KP], BF16, name="x_grouped", bufs=3, align_bytes=64)
-            for b in banks:
-                acc = bank()
-                for g in range(2 * b, 2 * b + 2):
-                    if g == 0:
-                        words = xo_sb[i][:].bitcast(F32)
-                    else:
-                        words = xr_sb[i][:, (g - 1) * KP : g * KP].bitcast(F32)
-                    for u in range(2):
-                        slot = 2 * (g % 2) + u
-                        nc.tensor.transpose(acc[:, slot * P : (slot + 1) * P], words[:, u : 2 * P : 2], ident32[:])
-                copy_words_out(x_grouped[i][:, 2 * b * KP : 2 * (b + 1) * KP], acc)
+        def as_words(ap):
+            return ap.bitcast(F32).rearrange("p (g r u) -> p g r u", r=P, u=2)
+
+        def turn_x(i, part):
+            if part == 0:
+                x_grouped[i] = work.tile([P, X_GROUPS * GROUP], BF16, name="x_grouped", bufs=3, align_bytes=64)
+            acc = next_bank()
+            for g in (2 * part, 2 * part + 1):
+                source = xo_sb[i][:] if g == 0 else xr_sb[i][:, (g - 1) * GROUP : g * GROUP]
+                words = source.bitcast(F32)
+                for u in range(2):
+                    place = 2 * (g % 2) + u
+                    nc.tensor.transpose(acc[:, place * P : (place + 1) * P], words[:, u : 2 * P : 2], ident[:])
+            words_out(nc.scalar.copy, as_words(x_grouped[i][:, 2 * part * GROUP : 2 * (part + 1) * GROUP]), acc, 0, 2)
 
         def quantize_x(i):
-            x_codes[i] = work.tile([P, XG * P], U32, name="x_codes", bufs=3, align_bytes=64)
-            x_plane[i] = work.tile([P, XG * P], U8, name="x_plane", bufs=3, align_bytes=64)
+            x_codes[i] = work.tile([P, X_GROUPS * P], U32, name="x_codes", bufs=3, align_bytes=64)
+            x_plane[i] = work.tile([P, X_GROUPS * P], U8, name="x_plane", bufs=3, align_bytes=64)
             nc.vector.quantize_mx(out=x_codes[i][:].bitcast(FP8X4), scales=x_plane[i][:], in_=x_grouped[i][:])
 
-        def project_pass(i, h, n):
+        def project_pass(i, f, n):
             if n == 0:
-                u_acc[i, h] = psum.tile([P, BANK], F32, name="u_acc", tag="u_acc", bufs=UB)
-            g = (n + 1) % XG
+                u_acc[i, f] = psum.tile([P, BANK], F32, name="u_acc", tag="u_acc", bufs=2)
+            g = (n + 1) % X_GROUPS
             tok = slice(g * P, (g + 1) * P)
-            cols = slice(h * H, (h + 1) * H)
+            cols = slice(f * H, (f + 1) * H)
             if g == 0:
                 rhs, rhs_scale = wo_codes[:, cols].bitcast(FP8X4), wo_plane[:, cols]
             else:
-                rhs, rhs_scale = wr_codes[h][:, g - 1, :].bitcast(FP4X4), wr_plane[:, g - 1, cols]
+                rhs, rhs_scale = wr_codes[f][:, g - 1, :].bitcast(FP4X4), wr_plane[:, g - 1, cols]
             nc.tensor.matmul_mx(
-                out=u_acc[i, h][:],
+                out=u_acc[i, f][:],
                 lhsT=x_codes[i][:, tok].bitcast(FP8X4),
                 lhsT_scale=x_plane[i][:, tok],
                 rhs=rhs,
                 rhs_scale=rhs_scale,
                 start=(n == 0),
-                stop=(n == XG - 1),
+                stop=(n == X_GROUPS - 1),
             )
 
-        def project(i, h):
-            for n in range(XG):
-                project_pass(i, h, n)
-
-        def add_bias(i, h):
-            u_sorted[i, h] = work.tile([P, H], BF16, name="u_sorted", bufs=4)
+        def add_bias(i, f):
+            u_sorted[i, f] = work.tile([P, H], BF16, name="u_sorted", bufs=4)
             nc.vector.tensor_tensor(
-                out=u_sorted[i, h][:].rearrange("p (u k e) -> p u k e", u=2, e=2),
-                in0=u_acc[i, h][:].rearrange("p (k u e) -> p u k e", u=2, e=2),
-                in1=bias_bc[:, h * H : (h + 1) * H].rearrange("p (u k e) -> p u k e", u=2, e=2),
+                out=u_sorted[i, f][:].rearrange("p (u k e) -> p u k e", u=2, e=2),
+                in0=u_acc[i, f][:].rearrange("p (k u e) -> p u k e", u=2, e=2),
+                in1=bias_sorted[:, f * H : (f + 1) * H].rearrange("p (u k e) -> p u k e", u=2, e=2),
                 op=ALU.add,
             )
 
-        def turn_u(i, halves=(0, 1)):
-            acc = bank()
-            for h in halves:
-                words = u_sorted[i, h][:].bitcast(F32)
+        def turn_u(i, first=0, count=2):
+            acc = next_bank()
+            for f in range(first, first + count):
+                words = u_sorted[i, f][:].bitcast(F32)
                 for u in range(2):
-                    slot = 2 * h + u
-                    nc.tensor.transpose(acc[:, slot * P : (slot + 1) * P], words[:, u * P : (u + 1) * P], ident32[:])
-            if halves[0] == 0:
+                    place = 2 * f + u
+                    nc.tensor.transpose(acc[:, place * P : (place + 1) * P], words[:, u * P : (u + 1) * P], ident[:])
+            if first == 0:
                 u_grouped[i] = work.tile([P, Q], BF16, name="u_grouped", align_bytes=64)
-            lo, hi = halves[0], halves[-1] + 1
-            nc.scalar.copy(
-                out=u_grouped[i][:, lo * KP : hi * KP].bitcast(F32).rearrange("p (g r u) -> p g r u", r=P, u=2),
-                in_=acc[:, lo * 2 * P : hi * 2 * P].rearrange("p (g u r) -> p g r u", r=P, u=2),
-            )
+            dst = as_words(u_grouped[i][:, first * GROUP : (first + count) * GROUP])
+            words_out(nc.scalar.copy, dst, acc, first, count)
 
-        def quantize_u(i, halves=(0, 1)):
-            if halves[0] == 0:
+        def quantize_u(i, first=0, count=2):
+            if first == 0:
                 u_codes[i] = work.tile([P, 2 * P], U32, name="u_codes", bufs=3, align_bytes=64)
                 u_plane[i] = work.tile([P, 2 * P], U8, name="u_plane", bufs=3, align_bytes=64)
-            lo, hi = halves[0], halves[-1] + 1
+            tok = slice(first * P, (first + count) * P)
             nc.vector.quantize_mx(
-                out=u_codes[i][:, lo * P : hi * P].bitcast(FP8X4),
-                scales=u_plane[i][:, lo * P : hi * P],
-                in_=u_grouped[i][:, lo * KP : hi * KP],
+                out=u_codes[i][:, tok].bitcast(FP8X4),
+                scales=u_plane[i][:, tok],
+                in_=u_grouped[i][:, first * GROUP : (first + count) * GROUP],
             )
 
-        def gate(i, h, c, s):
-            if (i, h, s) not in gates:
-                gates[i, h, s] = work.tile([P, HALF], F32, name="gate%d" % s, bufs=3 + 2 * s)
-                (gate1, gate2)[s][i, h] = gates[i, h, s]
+        def score(step, n):
+            i, h = divmod(step, 2)
+            c, s = divmod(n, 2)
+            if c == 0:
+                gates[step, s] = work.tile([P, HALF], F32, name="gate%d" % s, bufs=(3, 5)[s])
             tok = slice(s * P, (s + 1) * P)
-            cols = slice(c * BANK, (c + 1) * BANK)
-            acc = bank()
+            acc = next_bank()
             nc.tensor.matmul_mx(
                 out=acc[:],
                 lhsT=u_codes[i][:, tok].bitcast(FP8X4),
                 lhsT_scale=u_plane[i][:, tok],
-                rhs=sub_codes[2 * s + h][:, cols].bitcast(FP8X4),
+                rhs=sub_codes[s, h][:, CHUNKS[c]].bitcast(FP8X4),
                 rhs_scale=sub_plane[4 * s :, h * HALF + c * BANK : h * HALF + (c + 1) * BANK],
                 start=True,
                 stop=True,
             )
-            nc.scalar.activation(out=gates[i, h, s][:, cols], in_=acc[:], func=ACT.Sigmoid)
+            nc.scalar.activation(out=gates[step, s][:, CHUNKS[c]], in_=acc[:], func=ACT.Sigmoid)
 
-        def score(i, h):
-            if i == 0:
-                return
-            for c in range(2):
-                for s in range(2):
-                    gate(i, h, c, s)
+        def multiply_gates(step, c):
+            first, second = gates[step, 0][:, CHUNKS[c]], gates[step, 1][:, CHUNKS[c]]
+            nc.vector.tensor_tensor(out=first, in0=first, in1=second, op=ALU.mult)
 
-        def multiply_gates(i, h, cols=slice(0, HALF)):
-            nc.vector.tensor_tensor(out=gate1[i, h][:, cols], in0=gate1[i, h][:, cols], in1=gate2[i, h][:, cols], op=ALU.mult)
+        def apply_gain(step, c):
+            if c == 0:
+                y_f32[step] = work.tile([P, HALF], F32, name="y_f32", bufs=4)
+            nc.vector.tensor_tensor(
+                out=y_f32[step][:, CHUNKS[c]].rearrange("p (n j e) -> p n j e", j=4, e=2),
+                in0=gates[step, 0][:, CHUNKS[c]].rearrange("p (n j e) -> p n j e", j=4, e=2),
+                in1=gain_psum[step % 2][:, c * BANK // 8 : (c + 1) * BANK // 8],
+                op=ALU.mult,
+            )
 
-        def apply_gain(i, h, cols=slice(0, HALF)):
-            if cols.start == 0:
-                y_f32[i, h] = work.tile([P, HALF], F32, name="y_f32", bufs=4)
-            nc.vector.tensor_tensor(out=y_f32[i, h][:, cols], in0=gate1[i, h][:, cols], in1=gain_of[h][:, cols], op=ALU.mult)
-            if (i, h) == (TILES - 1, 1):
-                nc.sync.dma_start(out=out_0[i * P : (i + 1) * P, h * HALF : (h + 1) * HALF][:, cols], in_=y_f32[i, h][:, cols])
-            elif cols.stop == HALF:
-                nc.sync.dma_start(out=out_0[i * P : (i + 1) * P, h * HALF : (h + 1) * HALF], in_=y_f32[i, h][:])
+        def store_y(step, cols=slice(0, HALF)):
+            i, h = divmod(step, 2)
+            nc.sync.dma_start(out=out_0[i * P : (i + 1) * P, h * HALF : (h + 1) * HALF][:, cols], in_=y_f32[step][:, cols])
 
-        def round_y(i, h, chunks, eng, into=None):
-            if chunks[0] == 0:
-                if into is None:
-                    own = work.tile([P, HALF], BF16, name="y_sorted", bufs=3)
-                    y_sorted[i, h] = own[:]
-                else:
-                    y_sorted[i, h] = into[:].bitcast(BF16)[:, 0:HALF]
-            ks = slice(chunks[0] * P, (chunks[-1] + 1) * P)
-            dst = y_sorted[i, h].rearrange("p (u k e) -> p u k e", u=2, e=2)[:, :, ks, :]
-            src = y_f32[i, h][:].rearrange("p (k u e) -> p u k e", u=2, e=2)[:, :, ks, :]
-            if eng == "pool":
-                nc.gpsimd.tensor_scalar(out=dst, in0=src, scalar1=1.0, scalar2=0.0, op0=ALU.mult, op1=ALU.add)
-            elif eng == "act":
-                nc.scalar.copy(out=dst, in_=src)
-            else:
-                nc.vector.tensor_copy(out=dst, in_=src)
+        def rounding_views(step, words):
+            dst = y_sorted[step].rearrange("p (u k e) -> p u k e", u=2, e=2)[:, :, words, :]
+            src = y_f32[step][:].rearrange("p (k u e) -> p u k e", u=2, e=2)[:, :, words, :]
+            return dst, src
 
-        def turn_y(i, h, chunks=(0, 1)):
-            acc = bank()
-            words = y_sorted[i, h].bitcast(F32)
-            for c in chunks:
+        def round_on_gpsimd(step):
+            y_sorted[step] = gates[step + 1, 1][:].bitcast(BF16)[:, 0:HALF]
+            dst, src = rounding_views(step, slice(0, 2 * P))
+            nc.gpsimd.tensor_scalar(out=dst, in0=src, scalar1=1.0, scalar2=0.0, op0=ALU.mult, op1=ALU.add)
+
+        def round_chunk(step, c, copy):
+            if c == 0:
+                own = work.tile([P, HALF], BF16, name="y_sorted", bufs=1)
+                y_sorted[step] = own[:]
+            dst, src = rounding_views(step, slice(c * P, (c + 1) * P))
+            copy(out=dst, in_=src)
+
+        def turn_y(step, first=0, count=2, copy=nc.scalar.copy):
+            i, h = divmod(step, 2)
+            acc = next_bank()
+            words = y_sorted[step].bitcast(F32)
+            for c in range(first, first + count):
                 for u in range(2):
-                    slot = 2 * c + u
-                    first = (2 * u + c) * P
-                    nc.tensor.transpose(acc[:, slot * P : (slot + 1) * P], words[:, first : first + P], ident32[:])
-            if chunks[0] == 0 and i % 2 == 0:
-                y_grouped[i // 2, h] = work.tile([P, 2, 2 * KP], BF16, name="y_grouped", bufs=3, align_bytes=64)
-            lo, hi = chunks[0], chunks[-1] + 1
-            nc.scalar.copy(
-                out=y_grouped[i // 2, h][:, lo:hi, (i % 2) * KP : (i % 2 + 1) * KP].bitcast(F32).rearrange("p g (r u) -> p g r u", u=2),
-                in_=acc[:, lo * 2 * P : hi * 2 * P].rearrange("p (g u r) -> p g r u", r=P, u=2),
-            )
+                    place, start = 2 * c + u, (2 * u + c) * P
+                    nc.tensor.transpose(acc[:, place * P : (place + 1) * P], words[:, start : start + P], ident[:])
+            if first == 0 and i % 2 == 0:
+                y_grouped[i // 2, h] = work.tile([P, 2, 2 * GROUP], BF16, name="y_grouped", bufs=3, align_bytes=64)
+            dst = y_grouped[i // 2, h][:, first : first + count, (i % 2) * GROUP : (i % 2 + 1) * GROUP]
+            words_out(copy, dst.bitcast(F32).rearrange("p g (r u) -> p g r u", u=2), acc, first, count)
 
-        def quantize_y(pair, h, c, tiles=(0, 1)):
-            if pair not in y_codes:
-                y_codes[pair] = work.tile([P, CHUNKS, 2 * P], U32, name="y_codes", align_bytes=64)
-                y_plane[pair] = work.tile([P, CHUNKS, 2 * P], U8, name="y_plane", align_bytes=64)
-            lo, hi = tiles[0], tiles[-1] + 1
+        def quantize_y(pair, g):
+            if g == 0:
+                y_codes[pair] = work.tile([P, E_GROUPS, 2 * P], U32, name="y_codes", align_bytes=64)
             nc.vector.quantize_mx(
-                out=y_codes[pair][:, 2 * h + c, lo * P : hi * P].bitcast(FP8X4),
-                scales=y_plane[pair][:, 2 * h + c, lo * P : hi * P],
-                in_=y_grouped[pair, h][:, c, lo * KP : hi * KP],
+                out=y_codes[pair][:, g, :].bitcast(FP8X4),
+                scales=y_plane[:, g, 2 * pair * P : 2 * (pair + 1) * P],
+                in_=y_grouped[pair, g // 2][:, g % 2, :],
             )
 
-        def store_words(pair, lo, hi):
+        def store_words(pair, first, count):
             tok = slice(2 * pair * P, 2 * (pair + 1) * P)
+            groups = slice(first, first + count)
             words = out_1.rearrange("g p m t -> p g (m t)").bitcast(I32)
-            nc.sync.dma_start(out=words[:, lo:hi, tok], in_=y_codes[pair][:, lo:hi, :].bitcast(I32))
+            nc.sync.dma_start(out=words[:, groups, tok], in_=y_codes[pair][:, groups, :].bitcast(I32))
 
-        def store_scales(pair, queues):
-            tok = slice(2 * pair * P, 2 * (pair + 1) * P)
-            for q in range(4):
-                queues[q % len(queues)].dma_start(
-                    out=out_2[:, 4 * q : 4 * q + 4, tok].rearrange("g r m -> r g m").bitcast(I32),
-                    in_=y_plane[pair][32 * q : 32 * q + 4, :, :].bitcast(I32),
+        def store_scales(tok, queues):
+            for quad in range(4):
+                queues[quad % len(queues)].dma_start(
+                    out=out_2[:, 4 * quad : 4 * quad + 4, tok].rearrange("g r m -> r g m").bitcast(I32),
+                    in_=y_plane[32 * quad : 32 * quad + 4, :, tok].bitcast(I32),
                 )
 
-        def live(i):
-            return 0 <= i < TILES
-
-        def finish(i, h):
-            if i % 2:
-                quantize_y(i // 2, h, 0)
-                quantize_y(i // 2, h, 1)
-                if h:
-                    store_words(i // 2, 0, CHUNKS)
-                    store_scales(i // 2, [nc.sync])
-
-        def at(lags, s):
-            return [j for j in range(TILES) if 2 * j - lags[j] == s]
-
-        def half(s):
-            return (s // 2, s % 2) if 0 <= s < 2 * TILES else None
+        def quantize_planes(step):
+            i, h = divmod(step, 2)
+            if i % 2 == 1:
+                quantize_y(i // 2, 2 * h)
+                quantize_y(i // 2, 2 * h + 1)
+                if h == 1:
+                    store_words(i // 2, 0, E_GROUPS)
+                    if i == TILES // 2 - 1:
+                        store_scales(slice(0, T // 2), [nc.sync])
 
         warm = keep.tile([P, 2], F32, name="warm")
-        nc.scalar.activation(out=warm[:], in_=ident32[:, 0:2], func=ACT.Sigmoid)
-        turn_x(0)
-        vec_cols = turn_vector(vec_rows)
-        spread_bias(vec_cols)
-        if GEARLY:
-            spread_gain(vec_cols)
+        nc.scalar.activation(out=warm[:], in_=ident[:, 0:2], func=ACT.Sigmoid)
+        turn_x(0, 0)
+        turn_x(0, 1)
+        spread_bias()
+        spread_gain()
         group_wo(0)
         quantize_x(0)
         quantize_wo(0)
         group_wo(1)
-        project(0, 0)
+        for n in range(X_GROUPS):
+            project_pass(0, 0, n)
         quantize_wo(1)
-        project(0, 1)
+        for n in range(X_GROUPS):
+            project_pass(0, 1, n)
         add_bias(0, 0)
-        if HEAD == 0:
-            turn_u(0, (0,))
-            add_bias(0, 1)
-            quantize_u(0, (0,))
-            turn_u(0, (1,))
-            gate(0, 0, 0, 0)
-            gate(0, 0, 1, 0)
-            quantize_u(0, (1,))
-            turn_x(1)
-            quantize_x(1)
-            gate(0, 1, 0, 0)
-            gate(0, 1, 1, 0)
-            gate(0, 0, 0, 1)
-            gate(0, 0, 1, 1)
-            if not GEARLY:
-                spread_gain(vec_cols)
-            project(1, 0)
-            add_bias(1, 0)
-            gate(0, 1, 0, 1)
-            gate(0, 1, 1, 1)
-        else:
-            turn_u(0, (0,))
-            add_bias(0, 1)
-            quantize_u(0, (0,))
-            turn_x(1, (0,))
-            turn_u(0, (1,))
-            turn_x(1, (1,))
-            quantize_u(0, (1,))
-            quantize_x(1)
-            gate(0, 0, 0, 0)
-            gate(0, 0, 1, 0)
-            gate(0, 0, 0, 1)
-            gate(0, 0, 1, 1)
-            if not GEARLY:
-                spread_gain(vec_cols)
+        turn_u(0, 0, 1)
+        add_bias(0, 1)
+        quantize_u(0, 0, 1)
+        turn_x(1, 0)
+        turn_u(0, 1, 1)
+        turn_x(1, 1)
+        quantize_u(0, 1, 1)
+        quantize_x(1)
+        for n in (0, 2, 1, 3):
+            score(0, n)
+        for n in range(4):
+            project_pass(1, 0, n)
+            score(1, n)
+        add_bias(1, 0)
+
+        def turn_x_step(i, part):
+            return max(2 * i - TURN_X_AHEAD[part], i - 2)
+
+        def project_step(i, f):
+            return max(2 * i - PROJECT_AHEAD[f], i) if i > 1 else 0
+
+        later_halves = [(i, f) for i in range(1, TILES) for f in range(2)][1:]
+        for step in range(STEPS - 1):
+            projected = [(i, f) for i, f in later_halves if project_step(i, f) == step]
+            passes = [(i, f, n) for i, f in projected for n in range(X_GROUPS)]
             for n in range(4):
-                project_pass(1, 0, n)
-                gate(0, 1, n // 2, n % 2)
-            add_bias(1, 0)
-        for s in range(FIRST, 2 * TILES - 1):
-            todo = [(j, 0, n) for j in at(SA, s) for n in range(XG)] + [(j, 1, n) for j in at(SB, s) for n in range(XG)]
-            per = len(todo) // 4
-            for n in range(4):
-                if s in S2FIRST and s > 1:
-                    gate(*half(s), n // 2, n % 2)
-                for job in todo[n * per : (n + 1) * per]:
+                for job in passes[n * len(projected) : (n + 1) * len(projected)]:
                     project_pass(*job)
-                if s not in S2FIRST and s > 1:
-                    gate(*half(s), n // 2, n % 2)
-            if POOL:
-                for step in DV:
-                    if step == "Y" and half(s - LY - 1):
-                        finish(*half(s - LY - 1))
-                    if step == "U":
-                        for j in at(UT, s - 1):
-                            if UT[j] > 1:
-                                quantize_u(j)
-                    if step == "X":
-                        for j in at(XB, s - 1):
-                            if XB[j] - SA[j] > 1:
-                                quantize_x(j)
-                    if step == "P" and half(s - 1):
-                        multiply_gates(*half(s - 1))
-                        if half(s - 2):
-                            round_y(*half(s - 2), (0, 1), "pool", gate2[half(s - 1)])
-                    if step == "B":
-                        for j in at(SA, s):
-                            add_bias(j, 0)
-                        for j in at(SB, s):
-                            add_bias(j, 1)
-                    if step == "G" and half(s - 1):
-                        apply_gain(*half(s - 1))
-            else:
-                if half(s - 1):
-                    multiply_gates(*half(s - 1))
-                for j in at(SA, s):
-                    add_bias(j, 0)
-                for j in at(SB, s):
-                    add_bias(j, 1)
-                for j in at(UT, s - 1):
-                    if UT[j] > 1:
-                        quantize_u(j)
-                for j in at(XB, s - 1):
-                    if XB[j] - SA[j] > 1:
-                        quantize_x(j)
-                on_act = ACT_CAST and (s % ACT_EVERY == 0 or s >= ACT_FROM)
-                if half(s - 1):
-                    apply_gain(*half(s - 1))
-                if half(s - LY - 1):
-                    finish(*half(s - LY - 1))
-                if half(s - 1):
-                    round_y(*half(s - 1), (0,) if on_act else (0, 1), "dve")
-            for j in at(UT, s):
-                if SB[j] > UT[j]:
-                    turn_u(j)
-            for j in at(XA, s):
-                turn_x(j, (0,))
-            for j in at(XB, s):
-                turn_x(j, (1,))
-            if s == GSLOT and not GDMA and not SHALLOW:
-                spread_gain(vec_cols)
-            if half(s - LY):
-                turn_y(*half(s - LY))
-            for j in at(UT, s):
-                if SB[j] == UT[j]:
-                    turn_u(j)
-            if not POOL and half(s - 1) and on_act:
-                round_y(*half(s - 1), (1,), "act")
-            for j in at(UT, s):
-                if UT[j] == 1:
-                    quantize_u(j)
-            for j in at(XB, s):
-                if XB[j] - SA[j] == 1:
-                    quantize_x(j)
-        last = TILES - 1
-        chunk = [slice(0, BANK), slice(BANK, HALF)]
-        score(last, 1)
+                if step > 1:
+                    score(step, n)
+            if step >= 1:
+                multiply_gates(step - 1, 0)
+                if step >= 2:
+                    round_on_gpsimd(step - 2)
+                multiply_gates(step - 1, 1)
+                apply_gain(step - 1, 0)
+                apply_gain(step - 1, 1)
+                store_y(step - 1)
+            for i in range(2, TILES):
+                if turn_x_step(i, 1) == step - 1:
+                    quantize_x(i)
+            for i in range(1, TILES):
+                if 2 * i - TURN_U_AHEAD == step - 1:
+                    quantize_u(i)
+            for i, f in projected:
+                add_bias(i, f)
+            if step > TURN_Y_BEHIND:
+                quantize_planes(step - TURN_Y_BEHIND - 1)
+            for i in range(2, TILES):
+                for part in range(2):
+                    if turn_x_step(i, part) == step:
+                        turn_x(i, part)
+            if step >= TURN_Y_BEHIND:
+                turn_y(step - TURN_Y_BEHIND)
+            for i in range(1, TILES):
+                if 2 * i - TURN_U_AHEAD == step:
+                    turn_u(i)
+
+        last, pair = STEPS - 1, TILES // 2 - 1
+        for n in range(4):
+            score(last, n)
+        multiply_gates(last - 1, 0)
+        round_on_gpsimd(last - 2)
+        multiply_gates(last - 1, 1)
+        turn_y(last - 3)
+        apply_gain(last - 1, 0)
+        apply_gain(last - 1, 1)
+        store_y(last - 1)
         multiply_gates(last, 0)
-        round_y(last - 1, 1, (0, 1), "pool", gate2[last, 0])
-        turn_y(last - 1, 0)
+        round_on_gpsimd(last - 1)
         apply_gain(last, 0)
-        multiply_gates(last, 1, chunk[0])
-        round_y(last, 0, (0, 1), "act")
-        turn_y(last - 1, 1)
-        quantize_y(last // 2 - 1, 1, 0)
-        apply_gain(last, 1, chunk[0])
-        multiply_gates(last, 1, chunk[1])
-        round_y(last, 1, (0,), "act")
-        quantize_y(last // 2 - 1, 1, 1)
-        store_words(last // 2 - 1, 0, CHUNKS)
-        store_scales(last // 2 - 1, [nc.sync])
-        apply_gain(last, 1, chunk[1])
-        turn_y(last, 0)
-        turn_y(last, 1, (0,))
-        round_y(last, 1, (1,), "dve")
-        turn_y(last, 1, (1,))
-        quantize_y(last // 2, 0, 0)
-        quantize_y(last // 2, 0, 1)
-        store_words(last // 2, 0, 2)
-        quantize_y(last // 2, 1, 0)
-        quantize_y(last // 2, 1, 1)
-        store_words(last // 2, 2, 4)
-        store_scales(last // 2, [nc.scalar, nc.sync])
+        store_y(last, CHUNKS[0])
+        turn_y(last - 2, copy=nc.vector.tensor_copy)
+        round_chunk(last, 0, nc.scalar.copy)
+        multiply_gates(last, 1)
+        quantize_y(pair - 1, 2)
+        apply_gain(last, 1)
+        store_y(last, CHUNKS[1])
+        quantize_y(pair - 1, 3)
+        store_words(pair - 1, 0, E_GROUPS)
+        round_chunk(last, 1, nc.vector.tensor_copy)
+        turn_y(last - 1)
+        turn_y(last, 0, 1)
+        turn_y(last, 1, 1)
+        quantize_y(pair, 0)
+        quantize_y(pair, 1)
+        store_words(pair, 0, 2)
+        quantize_y(pair, 2)
+        quantize_y(pair, 3)
+        store_words(pair, 2, 2)
+        store_scales(slice(T // 2, T), [nc.scalar, nc.sync])

from contextlib import ExitStack

import concourse.mybir as mybir
from concourse.masks import make_identity

T, DO, DR, Q, H, N = 1024, 512, 1536, 1024, 512, 2048
FLOPS = 2 * T * (DO + DR) * Q + 2 * T * Q * N

F32 = mybir.dt.float32
BF16 = mybir.dt.bfloat16
I32 = mybir.dt.int32
U32 = mybir.dt.uint32
U8 = mybir.dt.uint8
FP8X4 = mybir.dt.float8_e4m3fn_x4
FP4X4 = mybir.dt.float4_e2m1fn_x4
ALU = mybir.AluOpType
ACT = mybir.ActivationFunctionType

P = 128
GROUP = 512
BANK = 512
TILES = T // P
X_GROUPS = (DO + DR) // GROUP
E_GROUPS = N // GROUP
HALF = N // 2
STEPS = 2 * TILES
CHUNKS = (slice(0, BANK), slice(BANK, HALF))

TURN_X_AHEAD = (7, 6)
PROJECT_AHEAD = (4, 3)
TURN_U_AHEAD = 2
TURN_Y_BEHIND = 3


def tile_paired_subkey_router_k6_kernel(
    tc, xo, xr, wo, wr_words, wr_scales, bq, sub_words, sub_scales, gain, out_0, out_1, out_2
):
    nc = tc.nc
    with ExitStack() as ctx:
        keep = ctx.enter_context(tc.tile_pool(name="keep", bufs=1))
        work = ctx.enter_context(tc.tile_pool(name="work", bufs=2))
        psum = ctx.enter_context(tc.psum_pool(name="psum", bufs=1))
        ctx.enter_context(tc.manual_schedule())

        def next_bank():
            return psum.tile([P, BANK], F32, name="bank", tag="bank", bufs=4)

        wr_plane = keep.tile([P, X_GROUPS - 1, Q], U8, name="wr_plane", align_bytes=64)
        sub_plane = keep.tile([P, N], U8, name="sub_plane", align_bytes=64)
        nc.vector.memset(wr_plane[:].rearrange("p g n -> p (g n)").bitcast(I32), 0)
        nc.vector.memset(sub_plane[:].bitcast(I32), 0)

        ident = keep.tile([P, P], F32, name="ident")
        make_identity(nc, ident[:])
        bias_rows = keep.tile([P, 8], BF16, name="bias_rows")
        gain_rows = keep.tile([P, 2, 8], BF16, name="gain_rows")
        nc.gpsimd.dma_start(out=bias_rows[:], in_=bq.rearrange("(n j) -> n j", j=8))
        nc.gpsimd.dma_start(out=gain_rows[:], in_=gain.rearrange("(h n j) -> n h j", h=2, j=8))

        xo_sb = [keep.tile([P, DO], BF16, name="xo%d" % i) for i in range(TILES)]
        xr_sb = [keep.tile([P, DR], BF16, name="xr%d" % i) for i in range(TILES)]
        wo_raw = [keep.tile([P, 4, H], BF16, name="wo_raw%d" % f) for f in range(2)]
        wr_codes = [keep.tile([P, X_GROUPS - 1, 2 * H], U8, name="wr_codes%d" % f, align_bytes=64) for f in range(2)]
        sub_codes = {}
        for s in range(2):
            for h in range(2):
                sub_codes[s, h] = keep.tile([P, HALF], U32, name="sub_codes%d%d" % (s, h), align_bytes=64)

        def load_x(i):
            rows = slice(i * P, (i + 1) * P)
            nc.sync.dma_start(out=xo_sb[i][:], in_=xo[rows, :])
            nc.sync.dma_start(out=xr_sb[i][:], in_=xr[rows, :])

        def load_w(f):
            nc.sync.dma_start(out=wo_raw[f][:], in_=wo[:, f * H : (f + 1) * H].rearrange("(p j) n -> p j n", j=4))
            nc.sync.dma_start(
                out=wr_codes[f][:].bitcast(I32),
                in_=wr_words[:, :, 2 * H * f : 2 * H * (f + 1)].rearrange("g p b -> p g b").bitcast(I32),
            )

        def load_sub(s, h):
            cols = sub_words[s].rearrange("p n t -> p (n t)")[:, 4 * HALF * h : 4 * HALF * (h + 1)]
            nc.sync.dma_start(out=sub_codes[s, h][:].bitcast(I32), in_=cols.bitcast(I32))

        load_x(0)
        load_w(0)
        for quad in range(4):
            nc.sync.dma_start(
                out=wr_plane[32 * quad : 32 * quad + 4, :, :].bitcast(I32),
                in_=wr_scales[:, 4 * quad : 4 * quad + 4, :].rearrange("g r n -> r g n").bitcast(I32),
            )
        load_w(1)
        load_x(1)
        load_sub(0, 0)
        for quad in range(4):
            nc.sync.dma_start(
                out=sub_plane[32 * quad : 32 * quad + 8, :].bitcast(I32),
                in_=sub_scales[:, 4 * quad : 4 * quad + 4, :].bitcast(I32),
            )
        load_sub(1, 0)
        load_sub(0, 1)
        load_sub(1, 1)
        for i in range(2, TILES):
            load_x(i)

        bias_sorted = keep.tile([P, Q], BF16, name="bias_sorted")
        gain_psum = []

        def spread(rows, acc):
            words = rows.bitcast(F32)
            for j in range(4):
                nc.tensor.transpose(acc[:, j * P : (j + 1) * P], words[:, j : j + 1].to_broadcast([P, P]), ident[:])

        def spread_bias():
            acc = next_bank()
            spread(bias_rows[:], acc)
            for f in range(2):
                nc.scalar.copy(
                    out=bias_sorted[:, f * H : (f + 1) * H].bitcast(F32).rearrange("p (u n a) -> p u n a", u=2, a=2),
                    in_=acc[:].rearrange("p (a u n) -> p u n a", a=2, u=2)[:, :, f * P // 2 : (f + 1) * P // 2, :],
                )

        def spread_gain():
            for h in range(2):
                acc = psum.tile([P, BANK], F32, name="gain_acc", tag="gain_acc", bufs=2)
                spread(gain_rows[:, h, :], acc)
                gain_psum.append(acc[:].bitcast(BF16).rearrange("p (j n e) -> p n j e", j=4, e=2))

        wo_codes = keep.tile([P, Q], U32, name="wo_codes", align_bytes=64)
        wo_plane = keep.tile([P, Q], U8, name="wo_plane", align_bytes=64)
        wo_grouped = [keep.tile([P, 4 * H], BF16, name="wo_grouped%d" % f, align_bytes=64) for f in range(2)]

        def group_wo(f):
            nc.vector.tensor_copy(
                out=wo_grouped[f][:].rearrange("p (c i j) -> p c j i", i=4, j=4),
                in_=wo_raw[f][:].rearrange("p j (c i) -> p c j i", i=4),
            )

        def quantize_wo(f):
            cols = slice(f * H, (f + 1) * H)
            nc.vector.quantize_mx(out=wo_codes[:, cols].bitcast(FP8X4), scales=wo_plane[:, cols], in_=wo_grouped[f][:])

        x_grouped, x_codes, x_plane = {}, {}, {}
        u_acc, u_sorted, u_grouped, u_codes, u_plane = {}, {}, {}, {}, {}
        gates, y_f32, y_sorted, y_grouped, y_codes = {}, {}, {}, {}, {}
        y_plane = keep.tile([P, E_GROUPS, T], U8, name="y_plane", align_bytes=64)

        def words_out(copy, dst, acc, first, count):
            copy(out=dst, in_=acc[:, first * 2 * P : (first + count) * 2 * P].rearrange("p (g u r) -> p g r u", r=P, u=2))

        def as_words(ap):
            return ap.bitcast(F32).rearrange("p (g r u) -> p g r u", r=P, u=2)

        def turn_x(i, part):
            if part == 0:
                x_grouped[i] = work.tile([P, X_GROUPS * GROUP], BF16, name="x_grouped", bufs=3, align_bytes=64)
            acc = next_bank()
            for g in (2 * part, 2 * part + 1):
                source = xo_sb[i][:] if g == 0 else xr_sb[i][:, (g - 1) * GROUP : g * GROUP]
                words = source.bitcast(F32)
                for u in range(2):
                    place = 2 * (g % 2) + u
                    nc.tensor.transpose(acc[:, place * P : (place + 1) * P], words[:, u : 2 * P : 2], ident[:])
            words_out(nc.scalar.copy, as_words(x_grouped[i][:, 2 * part * GROUP : 2 * (part + 1) * GROUP]), acc, 0, 2)

        def quantize_x(i):
            x_codes[i] = work.tile([P, X_GROUPS * P], U32, name="x_codes", bufs=3, align_bytes=64)
            x_plane[i] = work.tile([P, X_GROUPS * P], U8, name="x_plane", bufs=3, align_bytes=64)
            nc.vector.quantize_mx(out=x_codes[i][:].bitcast(FP8X4), scales=x_plane[i][:], in_=x_grouped[i][:])

        def project_pass(i, f, n):
            if n == 0:
                u_acc[i, f] = psum.tile([P, BANK], F32, name="u_acc", tag="u_acc", bufs=2)
            g = (n + 1) % X_GROUPS
            tok = slice(g * P, (g + 1) * P)
            cols = slice(f * H, (f + 1) * H)
            if g == 0:
                rhs, rhs_scale = wo_codes[:, cols].bitcast(FP8X4), wo_plane[:, cols]
            else:
                rhs, rhs_scale = wr_codes[f][:, g - 1, :].bitcast(FP4X4), wr_plane[:, g - 1, cols]
            nc.tensor.matmul_mx(
                out=u_acc[i, f][:],
                lhsT=x_codes[i][:, tok].bitcast(FP8X4),
                lhsT_scale=x_plane[i][:, tok],
                rhs=rhs,
                rhs_scale=rhs_scale,
                start=(n == 0),
                stop=(n == X_GROUPS - 1),
            )

        def add_bias(i, f):
            u_sorted[i, f] = work.tile([P, H], BF16, name="u_sorted", bufs=4)
            nc.vector.tensor_tensor(
                out=u_sorted[i, f][:].rearrange("p (u k e) -> p u k e", u=2, e=2),
                in0=u_acc[i, f][:].rearrange("p (k u e) -> p u k e", u=2, e=2),
                in1=bias_sorted[:, f * H : (f + 1) * H].rearrange("p (u k e) -> p u k e", u=2, e=2),
                op=ALU.add,
            )

        def turn_u(i, first=0, count=2):
            acc = next_bank()
            for f in range(first, first + count):
                words = u_sorted[i, f][:].bitcast(F32)
                for u in range(2):
                    place = 2 * f + u
                    nc.tensor.transpose(acc[:, place * P : (place + 1) * P], words[:, u * P : (u + 1) * P], ident[:])
            if first == 0:
                u_grouped[i] = work.tile([P, Q], BF16, name="u_grouped", align_bytes=64)
            dst = as_words(u_grouped[i][:, first * GROUP : (first + count) * GROUP])
            words_out(nc.scalar.copy, dst, acc, first, count)

        def quantize_u(i, first=0, count=2):
            if first == 0:
                u_codes[i] = work.tile([P, 2 * P], U32, name="u_codes", bufs=3, align_bytes=64)
                u_plane[i] = work.tile([P, 2 * P], U8, name="u_plane", bufs=3, align_bytes=64)
            tok = slice(first * P, (first + count) * P)
            nc.vector.quantize_mx(
                out=u_codes[i][:, tok].bitcast(FP8X4),
                scales=u_plane[i][:, tok],
                in_=u_grouped[i][:, first * GROUP : (first + count) * GROUP],
            )

        def score(step, n):
            i, h = divmod(step, 2)
            c, s = divmod(n, 2)
            if c == 0:
                gates[step, s] = work.tile([P, HALF], F32, name="gate%d" % s, bufs=(3, 5)[s])
            tok = slice(s * P, (s + 1) * P)
            acc = next_bank()
            nc.tensor.matmul_mx(
                out=acc[:],
                lhsT=u_codes[i][:, tok].bitcast(FP8X4),
                lhsT_scale=u_plane[i][:, tok],
                rhs=sub_codes[s, h][:, CHUNKS[c]].bitcast(FP8X4),
                rhs_scale=sub_plane[4 * s :, h * HALF + c * BANK : h * HALF + (c + 1) * BANK],
                start=True,
                stop=True,
            )
            nc.scalar.activation(out=gates[step, s][:, CHUNKS[c]], in_=acc[:], func=ACT.Sigmoid)

        def multiply_gates(step, c):
            first, second = gates[step, 0][:, CHUNKS[c]], gates[step, 1][:, CHUNKS[c]]
            nc.vector.tensor_tensor(out=first, in0=first, in1=second, op=ALU.mult)

        def apply_gain(step, c):
            if c == 0:
                y_f32[step] = work.tile([P, HALF], F32, name="y_f32", bufs=4)
            nc.vector.tensor_tensor(
                out=y_f32[step][:, CHUNKS[c]].rearrange("p (n j e) -> p n j e", j=4, e=2),
                in0=gates[step, 0][:, CHUNKS[c]].rearrange("p (n j e) -> p n j e", j=4, e=2),
                in1=gain_psum[step % 2][:, c * BANK // 8 : (c + 1) * BANK // 8],
                op=ALU.mult,
            )

        def store_y(step, cols=slice(0, HALF)):
            i, h = divmod(step, 2)
            nc.sync.dma_start(out=out_0[i * P : (i + 1) * P, h * HALF : (h + 1) * HALF][:, cols], in_=y_f32[step][:, cols])

        def rounding_views(step, words):
            dst = y_sorted[step].rearrange("p (u k e) -> p u k e", u=2, e=2)[:, :, words, :]
            src = y_f32[step][:].rearrange("p (k u e) -> p u k e", u=2, e=2)[:, :, words, :]
            return dst, src

        def round_on_gpsimd(step):
            y_sorted[step] = gates[step + 1, 1][:].bitcast(BF16)[:, 0:HALF]
            dst, src = rounding_views(step, slice(0, 2 * P))
            nc.gpsimd.tensor_scalar(out=dst, in0=src, scalar1=1.0, scalar2=0.0, op0=ALU.mult, op1=ALU.add)

        def round_chunk(step, c, copy):
            if c == 0:
                own = work.tile([P, HALF], BF16, name="y_sorted", bufs=1)
                y_sorted[step] = own[:]
            dst, src = rounding_views(step, slice(c * P, (c + 1) * P))
            copy(out=dst, in_=src)

        def turn_y(step, first=0, count=2, copy=nc.scalar.copy):
            i, h = divmod(step, 2)
            acc = next_bank()
            words = y_sorted[step].bitcast(F32)
            for c in range(first, first + count):
                for u in range(2):
                    place, start = 2 * c + u, (2 * u + c) * P
                    nc.tensor.transpose(acc[:, place * P : (place + 1) * P], words[:, start : start + P], ident[:])
            if first == 0 and i % 2 == 0:
                y_grouped[i // 2, h] = work.tile([P, 2, 2 * GROUP], BF16, name="y_grouped", bufs=3, align_bytes=64)
            dst = y_grouped[i // 2, h][:, first : first + count, (i % 2) * GROUP : (i % 2 + 1) * GROUP]
            words_out(copy, dst.bitcast(F32).rearrange("p g (r u) -> p g r u", u=2), acc, first, count)

        def quantize_y(pair, g):
            if g == 0:
                y_codes[pair] = work.tile([P, E_GROUPS, 2 * P], U32, name="y_codes", align_bytes=64)
            nc.vector.quantize_mx(
                out=y_codes[pair][:, g, :].bitcast(FP8X4),
                scales=y_plane[:, g, 2 * pair * P : 2 * (pair + 1) * P],
                in_=y_grouped[pair, g // 2][:, g % 2, :],
            )

        def store_words(pair, first, count):
            tok = slice(2 * pair * P, 2 * (pair + 1) * P)
            groups = slice(first, first + count)
            words = out_1.rearrange("g p m t -> p g (m t)").bitcast(I32)
            nc.sync.dma_start(out=words[:, groups, tok], in_=y_codes[pair][:, groups, :].bitcast(I32))

        def store_scales(tok, queues):
            for quad in range(4):
                queues[quad % len(queues)].dma_start(
                    out=out_2[:, 4 * quad : 4 * quad + 4, tok].rearrange("g r m -> r g m").bitcast(I32),
                    in_=y_plane[32 * quad : 32 * quad + 4, :, tok].bitcast(I32),
                )

        def quantize_planes(step):
            i, h = divmod(step, 2)
            if i % 2 == 1:
                quantize_y(i // 2, 2 * h)
                quantize_y(i // 2, 2 * h + 1)
                if h == 1:
                    store_words(i // 2, 0, E_GROUPS)
                    if i == TILES // 2 - 1:
                        store_scales(slice(0, T // 2), [nc.sync])

        warm = keep.tile([P, 2], F32, name="warm")
        nc.scalar.activation(out=warm[:], in_=ident[:, 0:2], func=ACT.Sigmoid)
        turn_x(0, 0)
        turn_x(0, 1)
        spread_bias()
        spread_gain()
        group_wo(0)
        quantize_x(0)
        quantize_wo(0)
        group_wo(1)
        for n in range(X_GROUPS):
            project_pass(0, 0, n)
        quantize_wo(1)
        for n in range(X_GROUPS):
            project_pass(0, 1, n)
        add_bias(0, 0)
        turn_u(0, 0, 1)
        add_bias(0, 1)
        quantize_u(0, 0, 1)
        turn_x(1, 0)
        turn_u(0, 1, 1)
        turn_x(1, 1)
        quantize_u(0, 1, 1)
        quantize_x(1)
        for n in (0, 2, 1, 3):
            score(0, n)
        for n in range(4):
            project_pass(1, 0, n)
            score(1, n)
        add_bias(1, 0)

        def turn_x_step(i, part):
            return max(2 * i - TURN_X_AHEAD[part], i - 2)

        def project_step(i, f):
            return max(2 * i - PROJECT_AHEAD[f], i) if i > 1 else 0

        later_halves = [(i, f) for i in range(1, TILES) for f in range(2)][1:]
        for step in range(STEPS - 1):
            projected = [(i, f) for i, f in later_halves if project_step(i, f) == step]
            passes = [(i, f, n) for i, f in projected for n in range(X_GROUPS)]
            for n in range(4):
                for job in passes[n * len(projected) : (n + 1) * len(projected)]:
                    project_pass(*job)
                if step > 1:
                    score(step, n)
            if step >= 1:
                multiply_gates(step - 1, 0)
                if step >= 2:
                    round_on_gpsimd(step - 2)
                multiply_gates(step - 1, 1)
                apply_gain(step - 1, 0)
                apply_gain(step - 1, 1)
                store_y(step - 1)
            for i in range(2, TILES):
                if turn_x_step(i, 1) == step - 1:
                    quantize_x(i)
            for i in range(1, TILES):
                if 2 * i - TURN_U_AHEAD == step - 1:
                    quantize_u(i)
            for i, f in projected:
                add_bias(i, f)
            if step > TURN_Y_BEHIND:
                quantize_planes(step - TURN_Y_BEHIND - 1)
            for i in range(2, TILES):
                for part in range(2):
                    if turn_x_step(i, part) == step:
                        turn_x(i, part)
            if step >= TURN_Y_BEHIND:
                turn_y(step - TURN_Y_BEHIND)
            for i in range(1, TILES):
                if 2 * i - TURN_U_AHEAD == step:
                    turn_u(i)

        last, pair = STEPS - 1, TILES // 2 - 1
        for n in range(4):
            score(last, n)
        multiply_gates(last - 1, 0)
        round_on_gpsimd(last - 2)
        multiply_gates(last - 1, 1)
        turn_y(last - 3)
        apply_gain(last - 1, 0)
        apply_gain(last - 1, 1)
        store_y(last - 1)
        multiply_gates(last, 0)
        round_on_gpsimd(last - 1)
        apply_gain(last, 0)
        store_y(last, CHUNKS[0])
        turn_y(last - 2, copy=nc.vector.tensor_copy)
        round_chunk(last, 0, nc.scalar.copy)
        multiply_gates(last, 1)
        quantize_y(pair - 1, 2)
        apply_gain(last, 1)
        store_y(last, CHUNKS[1])
        quantize_y(pair - 1, 3)
        store_words(pair - 1, 0, E_GROUPS)
        round_chunk(last, 1, nc.vector.tensor_copy)
        turn_y(last - 1)
        turn_y(last, 0, 1)
        turn_y(last, 1, 1)
        quantize_y(pair, 0)
        quantize_y(pair, 1)
        store_words(pair, 0, 2)
        quantize_y(pair, 2)
        quantize_y(pair, 3)
        store_words(pair, 2, 2)
        store_scales(slice(T // 2, T), [nc.scalar, nc.sync])
